import numpy as np
import ml_dtypes


def mxq(x, axis, fmt="e4m3"):
    dtype, down = {"e4m3": (ml_dtypes.float8_e4m3fn, 7), "e5m2": (ml_dtypes.float8_e5m2, 14)}[fmt]
    v = np.moveaxis(np.asarray(x, np.float32).astype(ml_dtypes.bfloat16).astype(np.float64), axis, -1)
    blocks = v.reshape(v.shape[:-1] + (-1, 32))
    amax = np.abs(blocks).max(-1, keepdims=True)
    byte = np.maximum(np.where(amax > 0, np.frexp(amax)[1] - 1 + 127, 0) - down, 1)
    scale = np.exp2(byte - 127.0)
    codes = (blocks / scale).astype(np.float32).astype(dtype).astype(np.float64)
    return np.moveaxis((codes * scale).reshape(v.shape), -1, axis)


WIDE = False


def mx_kscale(k):
    if not WIDE:
        return np.ones(k)
    levels = np.array([10, -10, 5, -5, 0])
    if k % 512:
        return np.exp2(np.random.permutation(np.resize(levels, k // 32))).repeat(32)
    a = np.empty((k // 512, 16))
    for p in range(k // 512):
        a[p, :8] = np.random.permutation(np.resize(levels, 8))
        for g in range(8):
            far = levels[np.abs(levels - a[p, g]) >= 10]
            a[p, g + 8] = far[np.random.randint(len(far))]
    return np.exp2(a.ravel()).repeat(32)


def f64(x):
    return np.asarray(x).astype(np.float64)


def striped(idx):
    return np.tile(idx.reshape(-1, 16).T, (8, 1)).astype(np.uint16)


def unstriped(offs):
    return offs[:16].T.reshape(-1).astype(np.int64)


def pack_weight(w):
    k, n = w.shape
    w = f64(np.asarray(w, np.float32).astype(ml_dtypes.bfloat16)).reshape(k // 32, 32, n)
    amax = np.abs(w).max(1)
    byte = np.clip(np.where(amax > 0, np.frexp(amax)[1] - 1 + 127 - 7, 1), 1, 254)
    scaled = (w * np.exp2(127.0 - byte)[:, None, :]).reshape(k, n).astype(np.float32)
    words = np.ascontiguousarray(scaled.reshape(k // 512, 128, 4, n).transpose(0, 1, 3, 2)).astype(ml_dtypes.float8_e4m3fn).view(np.uint8)
    return words, np.ascontiguousarray(byte.astype(np.uint8).reshape(k // 512, 16, n))


def unpack_weight(words, scales):
    g, p, n, _ = words.shape
    vals = np.ascontiguousarray(words).view(ml_dtypes.float8_e4m3fn).astype(np.float64) * np.repeat(np.exp2(scales.astype(np.float64) - 127.0), 8, axis=1)[..., None]
    return vals.transpose(0, 1, 3, 2).reshape(g * 512, n)


def relu(v):
    return np.maximum(v, 0.0)


K, T, S, H, N, U = 1024, 2048, 512, 512, 128, 1024


def setup_inputs():
    n = np.random.standard_normal
    s = mx_kscale(K)[:, None]
    u = mx_kscale(H)
    packed_xT = pack_weight(n((K, T)) * s)
    packed_w2 = pack_weight(n((H, N)) / np.sqrt(H) / u[:, None])
    return {
        "x_words": packed_xT[0],
        "x_scales": packed_xT[1],
        "w1": (n((K, H)) / np.sqrt(K) / s * u).astype(np.float32),
        "w2_words": packed_w2[0],
        "w2_scales": packed_w2[1],
        "skip": (n((H, U)) * u[:, None]).astype(np.float32),
        "offs": striped(np.random.permutation(T)[:S]),
        "cell": striped(np.random.permutation(U)[:S]),
    }


def reference(x_words, x_scales, w1, w2_words, w2_scales, skip, offs, cell):
    xq = unpack_weight(x_words, x_scales)[:, unstriped(offs)]
    up = np.zeros((H, U))
    up[:, unstriped(cell)] = relu(mxq(f64(w1), 0, "e4m3").T @ xq)
    z = up + f64(skip)
    return unpack_weight(w2_words, w2_scales).T @ mxq(z, 0, "e4m3")

@@ -1,0 +1,237 @@
+from contextlib import ExitStack
+
+import concourse.mybir as mybir
+from concourse.masks import make_identity
+
+K, T, S, H, N, U = 1024, 2048, 512, 512, 128, 1024
+FLOPS = 2 * K * H * S + 2 * H * N * U
+
+F32 = mybir.dt.float32
+BF16 = mybir.dt.bfloat16
+I32 = mybir.dt.int32
+U32 = mybir.dt.uint32
+U16 = mybir.dt.uint16
+U8 = mybir.dt.uint8
+FP8X4 = mybir.dt.float8_e4m3fn_x4
+ACT = mybir.ActivationFunctionType
+
+P = 128
+PASSES = K // 512
+TILES = H // P
+HALF = S // 2
+
+
+def tile_picked_unet_relu_p_kernel(
+    tc, x_words, x_scales, w1, w2_words, w2_scales, skip, offs, cell, out
+):
+    nc = tc.nc
+    with ExitStack() as ctx:
+        lists = ctx.enter_context(tc.tile_pool(name="lists", bufs=1))
+        sb = ctx.enter_context(tc.tile_pool(name="sb", bufs=1))
+        ps = ctx.enter_context(tc.psum_pool(name="ps", bufs=1))
+
+        offs_sb = lists.tile([P, S // 16], U16, name="offs_sb")
+        cell_sb = lists.tile([P, S // 16], U16, name="cell_sb")
+        x_table = [sb.tile([P, T], U32, name="x_table%d" % z) for z in range(PASSES)]
+        xs_table = sb.tile([P, T], U8, name="xs_table")
+        w1_raw = [
+            sb.tile([P, PASSES, 4, P], F32, name="w1_raw%d" % c, tag="slot%d" % c, align_bytes=64)
+            for c in range(TILES)
+        ]
+        skip_sb = [sb.tile([P, U], F32, name="skip_sb%d" % c) for c in range(TILES)]
+        up = [sb.tile([P, U], F32, name="up%d" % i) for i in range(2)]
+
+        def load_x(z, pieces):
+            words = x_words[z].rearrange("p n t -> p (n t)").bitcast(I32)
+            width = T // pieces
+            for i in range(pieces):
+                cols = slice(width * i, width * (i + 1))
+                nc.sync.dma_start(out=x_table[z][:, cols].bitcast(I32), in_=words[:, cols])
+
+        def load_w1(c):
+            for z in range(PASSES):
+                rows = w1[512 * z : 512 * (z + 1), P * c : P * (c + 1)]
+                nc.sync.dma_start(out=w1_raw[c][:, z, :, :], in_=rows.rearrange("(p j) m -> p j m", j=4))
+
+        nc.vector.memset(xs_table[:].bitcast(I32), 0)
+        nc.sync.dma_start(offs_sb[:], offs)
+        nc.sync.dma_start(cell_sb[:], cell)
+        load_w1(0)
+        load_x(0, 4)
+        for q in range(4):
+            nc.sync.dma_start(
+                out=xs_table[32 * q : 32 * q + 8, :].bitcast(I32), in_=x_scales[:, 4 * q : 4 * q + 4, :].bitcast(I32)
+            )
+        load_x(1, 1)
+        for c in range(1, TILES):
+            load_w1(c)
+        for c in range(TILES):
+            nc.sync.dma_start(out=skip_sb[c][:], in_=skip[P * c : P * (c + 1), :])
+
+        for i in range(2):
+            nc.vector.memset(up[i][:], 0.0)
+
+        ident = sb.tile([P, P], F32, name="ident")
+        make_identity(nc, ident[:])
+        w2_codes = sb.tile([P, 2, 2, N], U32, name="w2_codes", align_bytes=64)
+        w2_plane = sb.tile([P, 2, N], U8, name="w2_plane", align_bytes=64)
+        nc.gpsimd.memset(w2_codes[:].bitcast(I32), 0)
+        nc.gpsimd.memset(w2_plane[:].bitcast(I32), 0)
+        w2_rows = w2_words[0].rearrange("(h l) c t -> l h (c t)", h=2).bitcast(I32)
+        for s in range(2):
+            nc.sync.dma_start(out=w2_codes[64 * s : 64 * (s + 1), s, :, :].bitcast(I32), in_=w2_rows)
+        w2_srows = w2_scales[0].rearrange("(h a r) c -> a r h c", h=2, a=2)
+        for q in range(4):
+            nc.sync.dma_start(out=w2_plane[32 * q : 32 * q + 4, :, :].bitcast(I32), in_=w2_srows[q % 2].bitcast(I32))
+
+        w1_bf = [sb.tile([P, PASSES, P * 4], BF16, name="w1_bf%d" % c, align_bytes=64) for c in range(TILES)]
+        w1_codes = [sb.tile([P, PASSES * P], U32, name="w1_codes%d" % c, align_bytes=64) for c in range(TILES)]
+        w1_plane = [sb.tile([P, PASSES * P], U8, name="w1_plane%d" % c, align_bytes=64) for c in range(TILES)]
+
+        def cast_w1(c, z, on_vector):
+            dst = w1_bf[c][:, z, :].rearrange("p (g i j) -> p g j i", i=4, j=4)
+            src = w1_raw[c][:, z, :, :].rearrange("p j (g i) -> p g j i", i=4)
+            if on_vector:
+                nc.vector.tensor_copy(out=dst, in_=src)
+            else:
+                nc.scalar.activation(out=dst, in_=src, func=ACT.Copy)
+
+        def quantise_w1(c):
+            nc.vector.quantize_mx(
+                out=w1_codes[c][:].bitcast(FP8X4), scales=w1_plane[c][:], in_=w1_bf[c][:].rearrange("p z n -> p (z n)")
+            )
+
+        xg = [sb.tile([P, S], U32, name="xg%d" % z, align_bytes=64) for z in range(PASSES)]
+        xg_plane = sb.tile([P, S], U8, name="xg_plane", align_bytes=64)
+
+        cast_w1(0, 0, False)
+        cast_w1(0, 1, True)
+        quantise_w1(0)
+        nc.vector.tensor_copy(out=xg[0][:], in_=x_table[0][:].indirect(offs_sb[:]))
+        nc.vector.tensor_copy(out=xg_plane[:], in_=xs_table[:].indirect(offs_sb[:]))
+        for a in range(2):
+            nc.vector.tensor_copy(
+                out=xg[1][:, HALF * a : HALF * (a + 1)], in_=x_table[1][:].indirect(offs_sb[:, 16 * a : 16 * (a + 1)])
+            )
+
+        def first_product(c, a):
+            bank = ps.tile([P, 512], F32, name="h_bank", tag="pair%d_%d" % (c % 2, a))
+            cols = slice(HALF * a, HALF * (a + 1))
+            for z in range(PASSES):
+                nc.tensor.matmul_mx(
+                    out=bank[:, 0:HALF],
+                    lhsT=w1_codes[c][:, P * z : P * (z + 1)].bitcast(FP8X4),
+                    lhsT_scale=w1_plane[c][:, P * z : P * (z + 1)],
+                    rhs=xg[z][:, cols].bitcast(FP8X4),
+                    rhs_scale=xg_plane[4 * z : P, cols],
+                    start=(z == 0),
+                    stop=(z == PASSES - 1),
+                )
+            return bank
+
+        zt = [[sb.tile([P, 1024], BF16, name="zt%d_%d" % (g, a), align_bytes=64) for a in range(2)] for g in range(2)]
+
+        def turn_and_add(c):
+            for a in range(2):
+                bank = ps.tile([P, 4, P], F32, name="a_bank", tag="pair%d_%d" % ((c + 1) % 2 if c < 3 else 0, a))
+                for src, first in ((skip_sb[c], True), (up[c % 2], False)):
+                    for i in range(4):
+                        vb = 4 * (i % 2) + 2 * a + i // 2
+                        nc.tensor.matmul(
+                            bank[:, i, :],
+                            src[:, P * vb : P * (vb + 1)],
+                            ident[:],
+                            start=(first and i == 0),
+                            stop=(not first and i == 3),
+                            is_transpose=True,
+                        )
+                w0 = 32 * (c % 2)
+                dst = zt[c // 2][a][:].rearrange("p (u i w e) -> p i u w e", u=2, i=4, e=2)[:, :, :, w0 : w0 + 32, :]
+                src = bank[:].rearrange("p i (w u e) -> p i u w e", u=2, e=2)
+                if c == 3 and a == 1:
+                    nc.vector.tensor_copy(out=dst, in_=src)
+                else:
+                    nc.scalar.copy(out=dst, in_=src)
+
+        z_bf = [[sb.tile([P, 1024], BF16, name="z_bf%d_%d" % (g, a), align_bytes=64) for a in range(2)] for g in range(2)]
+
+        def turn_back(g, a):
+            bank = ps.tile([P, 2, 2, P], F32, name="b_bank", tag="back%d" % a)
+            words = zt[g][a][:].bitcast(F32)
+            for q in range(2):
+                for u in range(2):
+                    w0 = 256 * u + P * q
+                    nc.tensor.transpose(bank[:, q, u, :], words[:, w0 : w0 + P], ident[:])
+            dst = z_bf[g][a][:].bitcast(F32).rearrange("p (q v u) -> p q v u", q=2, u=2)
+            src = bank[:].rearrange("p q u v -> p q v u")
+            if g == 1 and a == 1:
+                nc.vector.tensor_copy(out=dst, in_=src)
+            else:
+                nc.scalar.copy(out=dst, in_=src)
+
+        h_first = sb.tile([P, HALF], F32, name="h_first")
+        bank = first_product(0, 0)
+        nc.scalar.activation(out=h_first[:], in_=bank[:, 0:HALF], func=ACT.Relu)
+        nc.vector.tensor_copy(out=up[0][:].indirect(cell_sb[:, 0:16]), in_=h_first[:])
+        bank = first_product(0, 1)
+        cast_w1(1, 0, False)
+        cast_w1(1, 1, False)
+        h_second = sb.tile([P, HALF], F32, name="h_second", tag="slot1", align_bytes=64)
+        nc.scalar.activation(out=h_second[:], in_=bank[:, 0:HALF], func=ACT.Relu)
+        quantise_w1(1)
+        nc.vector.tensor_copy(out=up[0][:].indirect(cell_sb[:, 16:32]), in_=h_second[:])
+
+        for c in range(1, TILES):
+            banks = [first_product(c, a) for a in range(2)]
+            if c + 1 < TILES:
+                cast_w1(c + 1, 0, False)
+                cast_w1(c + 1, 1, False)
+            h = sb.tile([P, S], F32, name="h", tag="slot%d" % (c + 1), align_bytes=64)
+            for a in range(2):
+                nc.scalar.activation(out=h[:, HALF * a : HALF * (a + 1)], in_=banks[a][:, 0:HALF], func=ACT.Relu)
+            if c + 1 < TILES:
+                quantise_w1(c + 1)
+            nc.vector.tensor_copy(out=up[c % 2][:].indirect(cell_sb[:]), in_=h[:])
+            if c == TILES - 1:
+                turn_back(0, 0)
+                turn_back(0, 1)
+            turn_and_add(c - 1)
+        turn_and_add(TILES - 1)
+
+        z_codes = [
+            sb.tile([P, 512], U32, name="z_codes0", tag="slot4", align_bytes=64),
+            sb.tile([P, 512], U32, name="z_codes1", align_bytes=64),
+        ]
+        z_plane = [sb.tile([P, 512], U8, name="z_plane%d" % g, align_bytes=64) for g in range(2)]
+        out_banks = [
+            [ps.tile([P, 512], F32, name="o_bank", tag=("out%d" % s if a == 0 else "pair1_%d" % s)) for s in range(2)]
+            for a in range(2)
+        ]
+
+        def second_product(g, a):
+            cols = slice(256 * a, 256 * (a + 1))
+            nc.vector.quantize_mx(out=z_codes[g][:, cols].bitcast(FP8X4), scales=z_plane[g][:, cols], in_=z_bf[g][a][:])
+            for s in range(2):
+                nc.tensor.matmul_mx(
+                    out=out_banks[a][s][:, 0:256],
+                    lhsT=w2_codes[:, s, g, :].bitcast(FP8X4),
+                    lhsT_scale=w2_plane[:, g, :],
+                    rhs=z_codes[g][:, cols].bitcast(FP8X4),
+                    rhs_scale=z_plane[g][:, cols],
+                    start=(g == 0),
+                    stop=(g == 1),
+                )
+
+        for a in range(2):
+            second_product(0, a)
+        out_view = out.rearrange("m (s a v) -> m a s v", s=2, a=2)
+        for a in range(2):
+            turn_back(1, a)
+            second_product(1, a)
+            res = sb.tile([P, 2, 256], F32, name="res%d" % a)
+            nc.scalar.copy(out=res[:, 0, :], in_=out_banks[a][0][:, 0:256])
+            if a == 0:
+                nc.scalar.copy(out=res[:, 1, :], in_=out_banks[a][1][:, 0:256])
+            else:
+                nc.vector.tensor_copy(out=res[:, 1, :], in_=out_banks[a][1][:, 0:256])
+            nc.sync.dma_start(out=out_view[:, a, :, :], in_=res[:])

@@ -30,16 +30,18 @@ def tile_picked_unet_relu_p_kernel(
         sb = ctx.enter_context(tc.tile_pool(name="sb", bufs=1))
         ps = ctx.enter_context(tc.psum_pool(name="ps", bufs=1))
 
+        def bank_tile(b, shape):
+            return ps.tile(shape, F32, name="bank%d" % b, tag="bank%d" % b)
+
         offs_sb = lists.tile([P, S // 16], U16, name="offs_sb")
         cell_sb = lists.tile([P, S // 16], U16, name="cell_sb")
         x_table = [sb.tile([P, T], U32, name="x_table%d" % z) for z in range(PASSES)]
         xs_table = sb.tile([P, T], U8, name="xs_table")
         w1_raw = [
-            sb.tile([P, PASSES, 4, P], F32, name="w1_raw%d" % c, tag="slot%d" % c, align_bytes=64)
-            for c in range(TILES)
+            sb.tile([P, PASSES, 4, P], F32, name="w1_raw%d" % c, tag="raw%d" % c, align_bytes=64) for c in range(TILES)
         ]
         skip_sb = [sb.tile([P, U], F32, name="skip_sb%d" % c) for c in range(TILES)]
-        up = [sb.tile([P, U], F32, name="up%d" % i) for i in range(2)]
+        up = [sb.tile([P, U], F32, name="up%d" % c) for c in range(TILES)]
 
         def load_x(z, pieces):
             words = x_words[z].rearrange("p n t -> p (n t)").bitcast(I32)
@@ -53,47 +55,59 @@ def tile_picked_unet_relu_p_kernel(
                 rows = w1[512 * z : 512 * (z + 1), P * c : P * (c + 1)]
                 nc.sync.dma_start(out=w1_raw[c][:, z, :, :], in_=rows.rearrange("(p j) m -> p j m", j=4))
 
+        def load_skip(c):
+            nc.sync.dma_start(out=skip_sb[c][:], in_=skip[P * c : P * (c + 1), :])
+
+        ident = sb.tile([P, P], F32, name="ident")
+        w2_codes = sb.tile([P, 2, 2, N], U32, name="w2_codes", align_bytes=64)
+        w2_plane = sb.tile([P, 2, N], U8, name="w2_plane", align_bytes=64)
+
+        def load_w2():
+            w2_rows = w2_words[0].rearrange("(h l) c t -> l h (c t)", h=2).bitcast(I32)
+            for s in range(2):
+                nc.sync.dma_start(out=w2_codes[64 * s : 64 * (s + 1), s, :, :].bitcast(I32), in_=w2_rows)
+            w2_srows = w2_scales[0].rearrange("(h a r) c -> a r h c", h=2, a=2)
+            for q in range(4):
+                nc.sync.dma_start(out=w2_plane[32 * q : 32 * q + 4, :, :].bitcast(I32), in_=w2_srows[q % 2].bitcast(I32))
+
         nc.vector.memset(xs_table[:].bitcast(I32), 0)
         nc.sync.dma_start(offs_sb[:], offs)
         nc.sync.dma_start(cell_sb[:], cell)
-        load_w1(0)
         load_x(0, 4)
+        load_w1(0)
         for q in range(4):
             nc.sync.dma_start(
                 out=xs_table[32 * q : 32 * q + 8, :].bitcast(I32), in_=x_scales[:, 4 * q : 4 * q + 4, :].bitcast(I32)
             )
-        load_x(1, 1)
-        for c in range(1, TILES):
-            load_w1(c)
-        for c in range(TILES):
-            nc.sync.dma_start(out=skip_sb[c][:], in_=skip[P * c : P * (c + 1), :])
-
-        for i in range(2):
-            nc.vector.memset(up[i][:], 0.0)
-
-        ident = sb.tile([P, P], F32, name="ident")
         make_identity(nc, ident[:])
-        w2_codes = sb.tile([P, 2, 2, N], U32, name="w2_codes", align_bytes=64)
-        w2_plane = sb.tile([P, 2, N], U8, name="w2_plane", align_bytes=64)
         nc.gpsimd.memset(w2_codes[:].bitcast(I32), 0)
         nc.gpsimd.memset(w2_plane[:].bitcast(I32), 0)
-        w2_rows = w2_words[0].rearrange("(h l) c t -> l h (c t)", h=2).bitcast(I32)
-        for s in range(2):
-            nc.sync.dma_start(out=w2_codes[64 * s : 64 * (s + 1), s, :, :].bitcast(I32), in_=w2_rows)
-        w2_srows = w2_scales[0].rearrange("(h a r) c -> a r h c", h=2, a=2)
-        for q in range(4):
-            nc.sync.dma_start(out=w2_plane[32 * q : 32 * q + 4, :, :].bitcast(I32), in_=w2_srows[q % 2].bitcast(I32))
+        load_x(1, 1)
+        load_w1(1)
+        load_skip(0)
+        load_w1(2)
+        load_skip(1)
+        load_w1(3)
+        load_skip(2)
+        load_skip(3)
+        load_w2()
+
+        for c in range(TILES):
+            nc.vector.memset(up[c][:], 0.0)
 
         w1_bf = [sb.tile([P, PASSES, P * 4], BF16, name="w1_bf%d" % c, align_bytes=64) for c in range(TILES)]
         w1_codes = [sb.tile([P, PASSES * P], U32, name="w1_codes%d" % c, align_bytes=64) for c in range(TILES)]
         w1_plane = [sb.tile([P, PASSES * P], U8, name="w1_plane%d" % c, align_bytes=64) for c in range(TILES)]
 
-        def cast_w1(c, z, on_vector):
-            dst = w1_bf[c][:, z, :].rearrange("p (g i j) -> p g j i", i=4, j=4)
-            src = w1_raw[c][:, z, :, :].rearrange("p j (g i) -> p g j i", i=4)
-            if on_vector:
-                nc.vector.tensor_copy(out=dst, in_=src)
-            else:
+        def cast_w1(c, whole):
+            if whole:
+                dst = w1_bf[c][:].rearrange("p z (g i j) -> p z g j i", i=4, j=4)
+                src = w1_raw[c][:].rearrange("p z j (g i) -> p z g j i", i=4)
+                nc.scalar.copy(out=dst, in_=src)
+                return
+            for z in range(PASSES):
+                dst = w1_bf[c][:, z, :].rearrange("p (g i j) -> p g j i", i=4, j=4)
+                src = w1_raw[c][:, z, :, :].rearrange("p j (g i) -> p g j i", i=4)
                 nc.scalar.activation(out=dst, in_=src, func=ACT.Copy)
 
         def quantise_w1(c):
@@ -104,22 +118,21 @@ def tile_picked_unet_relu_p_kernel(
         xg = [sb.tile([P, S], U32, name="xg%d" % z, align_bytes=64) for z in range(PASSES)]
         xg_plane = sb.tile([P, S], U8, name="xg_plane", align_bytes=64)
 
-        cast_w1(0, 0, False)
-        cast_w1(0, 1, True)
-        quantise_w1(0)
+        cast_w1(0, False)
         nc.vector.tensor_copy(out=xg[0][:], in_=x_table[0][:].indirect(offs_sb[:]))
         nc.vector.tensor_copy(out=xg_plane[:], in_=xs_table[:].indirect(offs_sb[:]))
+        quantise_w1(0)
         for a in range(2):
             nc.vector.tensor_copy(
                 out=xg[1][:, HALF * a : HALF * (a + 1)], in_=x_table[1][:].indirect(offs_sb[:, 16 * a : 16 * (a + 1)])
             )
 
         def first_product(c, a):
-            bank = ps.tile([P, 512], F32, name="h_bank", tag="pair%d_%d" % (c % 2, a))
+            bank = bank_tile(a, [P, HALF])
             cols = slice(HALF * a, HALF * (a + 1))
             for z in range(PASSES):
                 nc.tensor.matmul_mx(
-                    out=bank[:, 0:HALF],
+                    out=bank[:],
                     lhsT=w1_codes[c][:, P * z : P * (z + 1)].bitcast(FP8X4),
                     lhsT_scale=w1_plane[c][:, P * z : P * (z + 1)],
                     rhs=xg[z][:, cols].bitcast(FP8X4),
@@ -129,25 +142,39 @@ def tile_picked_unet_relu_p_kernel(
                 )
             return bank
 
-        zt = [[sb.tile([P, 1024], BF16, name="zt%d_%d" % (g, a), align_bytes=64) for a in range(2)] for g in range(2)]
+        def scatter(c, first, values):
+            count = values.shape[1]
+            nc.vector.tensor_copy(out=up[c][:].indirect(cell_sb[:, first // 16 : (first + count) // 16]), in_=values[:])
 
-        def turn_and_add(c):
+        zt = [
+            [sb.tile([P, 1024], BF16, name="zt%d_%d" % (g, a), tag="zt%d_%d" % (g, a), align_bytes=64) for a in range(2)]
+            for g in range(2)
+        ]
+
+        def turn(banks, src, first):
             for a in range(2):
-                bank = ps.tile([P, 4, P], F32, name="a_bank", tag="pair%d_%d" % ((c + 1) % 2 if c < 3 else 0, a))
-                for src, first in ((skip_sb[c], True), (up[c % 2], False)):
-                    for i in range(4):
-                        vb = 4 * (i % 2) + 2 * a + i // 2
-                        nc.tensor.matmul(
-                            bank[:, i, :],
-                            src[:, P * vb : P * (vb + 1)],
-                            ident[:],
-                            start=(first and i == 0),
-                            stop=(not first and i == 3),
-                            is_transpose=True,
-                        )
+                for i in range(4):
+                    vb = 4 * (i % 2) + 2 * a + i // 2
+                    nc.tensor.matmul(
+                        banks[a][:, i, :],
+                        src[:, P * vb : P * (vb + 1)],
+                        ident[:],
+                        start=(first and i == 0),
+                        stop=(not first and i == 3),
+                        is_transpose=True,
+                    )
+
+        def turn_skip(c, b):
+            banks = [bank_tile(b + a, [P, 4, P]) for a in range(2)]
+            turn(banks, skip_sb[c], True)
+            return banks
+
+        def turn_up(c, banks):
+            turn(banks, up[c], False)
+            for a in range(2):
                 w0 = 32 * (c % 2)
                 dst = zt[c // 2][a][:].rearrange("p (u i w e) -> p i u w e", u=2, i=4, e=2)[:, :, :, w0 : w0 + 32, :]
-                src = bank[:].rearrange("p i (w u e) -> p i u w e", u=2, e=2)
+                src = banks[a][:].rearrange("p i (w u e) -> p i u w e", u=2, e=2)
                 if c == 3 and a == 1:
                     nc.vector.tensor_copy(out=dst, in_=src)
                 else:
@@ -156,64 +183,27 @@ def tile_picked_unet_relu_p_kernel(
         z_bf = [[sb.tile([P, 1024], BF16, name="z_bf%d_%d" % (g, a), align_bytes=64) for a in range(2)] for g in range(2)]
 
         def turn_back(g, a):
-            bank = ps.tile([P, 2, 2, P], F32, name="b_bank", tag="back%d" % a)
+            bank = bank_tile(2 + a, [P, 2, 2, P])
             words = zt[g][a][:].bitcast(F32)
             for q in range(2):
                 for u in range(2):
                     w0 = 256 * u + P * q
                     nc.tensor.transpose(bank[:, q, u, :], words[:, w0 : w0 + P], ident[:])
             dst = z_bf[g][a][:].bitcast(F32).rearrange("p (q v u) -> p q v u", q=2, u=2)
-            src = bank[:].rearrange("p q u v -> p q v u")
-            if g == 1 and a == 1:
-                nc.vector.tensor_copy(out=dst, in_=src)
-            else:
-                nc.scalar.copy(out=dst, in_=src)
+            nc.scalar.copy(out=dst, in_=bank[:].rearrange("p q u v -> p q v u"))
 
-        h_first = sb.tile([P, HALF], F32, name="h_first")
-        bank = first_product(0, 0)
-        nc.scalar.activation(out=h_first[:], in_=bank[:, 0:HALF], func=ACT.Relu)
-        nc.vector.tensor_copy(out=up[0][:].indirect(cell_sb[:, 0:16]), in_=h_first[:])
-        bank = first_product(0, 1)
-        cast_w1(1, 0, False)
-        cast_w1(1, 1, False)
-        h_second = sb.tile([P, HALF], F32, name="h_second", tag="slot1", align_bytes=64)
-        nc.scalar.activation(out=h_second[:], in_=bank[:, 0:HALF], func=ACT.Relu)
-        quantise_w1(1)
-        nc.vector.tensor_copy(out=up[0][:].indirect(cell_sb[:, 16:32]), in_=h_second[:])
-
-        for c in range(1, TILES):
-            banks = [first_product(c, a) for a in range(2)]
-            if c + 1 < TILES:
-                cast_w1(c + 1, 0, False)
-                cast_w1(c + 1, 1, False)
-            h = sb.tile([P, S], F32, name="h", tag="slot%d" % (c + 1), align_bytes=64)
-            for a in range(2):
-                nc.scalar.activation(out=h[:, HALF * a : HALF * (a + 1)], in_=banks[a][:, 0:HALF], func=ACT.Relu)
-            if c + 1 < TILES:
-                quantise_w1(c + 1)
-            nc.vector.tensor_copy(out=up[c % 2][:].indirect(cell_sb[:]), in_=h[:])
-            if c == TILES - 1:
-                turn_back(0, 0)
-                turn_back(0, 1)
-            turn_and_add(c - 1)
-        turn_and_add(TILES - 1)
-
-        z_codes = [
-            sb.tile([P, 512], U32, name="z_codes0", tag="slot4", align_bytes=64),
-            sb.tile([P, 512], U32, name="z_codes1", align_bytes=64),
-        ]
+        z_codes = [sb.tile([P, 512], U32, name="z_codes%d" % g, align_bytes=64) for g in range(2)]
         z_plane = [sb.tile([P, 512], U8, name="z_plane%d" % g, align_bytes=64) for g in range(2)]
-        out_banks = [
-            [ps.tile([P, 512], F32, name="o_bank", tag=("out%d" % s if a == 0 else "pair1_%d" % s)) for s in range(2)]
-            for a in range(2)
-        ]
 
-        def second_product(g, a):
+        def quantise_z(g, a):
             cols = slice(256 * a, 256 * (a + 1))
             nc.vector.quantize_mx(out=z_codes[g][:, cols].bitcast(FP8X4), scales=z_plane[g][:, cols], in_=z_bf[g][a][:])
+
+        def second_product(g, a, banks):
+            cols = slice(256 * a, 256 * (a + 1))
             for s in range(2):
                 nc.tensor.matmul_mx(
-                    out=out_banks[a][s][:, 0:256],
+                    out=banks[s][:],
                     lhsT=w2_codes[:, s, g, :].bitcast(FP8X4),
                     lhsT_scale=w2_plane[:, g, :],
                     rhs=z_codes[g][:, cols].bitcast(FP8X4),
@@ -222,16 +212,50 @@ def tile_picked_unet_relu_p_kernel(
                     stop=(g == 1),
                 )
 
+        sum_bank = [4, 6, 4, 6]
+        sums = {}
+        for c in range(TILES - 1):
+            banks = [first_product(c, a) for a in range(2)]
+            h_a = sb.tile([P, HALF], F32, name="h_a%d" % c)
+            nc.scalar.activation(out=h_a[:], in_=banks[0][:], func=ACT.Relu)
+            scatter(c, 0, h_a)
+            cast_w1(c + 1, c == 0)
+            quantise_w1(c + 1)
+            h_b = sb.tile([P, HALF], F32, name="h_b%d" % c, tag="raw%d" % (c + 1), align_bytes=64)
+            nc.scalar.activation(out=h_b[:], in_=banks[1][:], func=ACT.Relu)
+            if c > 0:
+                turn_up(c - 1, sums[c - 1])
+            scatter(c, HALF, h_b)
+            if c < 2:
+                sums[c] = turn_skip(c, sum_bank[c])
+
+        c = TILES - 1
+        banks = [first_product(c, a) for a in range(2)]
+        h_last = sb.tile([P, S], F32, name="h_last")
         for a in range(2):
-            second_product(0, a)
+            nc.scalar.activation(out=h_last[:, HALF * a : HALF * (a + 1)], in_=banks[a][:], func=ACT.Relu)
+        scatter(c, 0, h_last)
+        for a in range(2):
+            turn_back(0, a)
+        sums[2] = turn_skip(2, sum_bank[2])
+        turn_up(2, sums[2])
+        sums[3] = turn_skip(3, sum_bank[3])
+        for a in range(2):
+            quantise_z(0, a)
+        turn_up(3, sums[3])
+
         out_view = out.rearrange("m (s a v) -> m a s v", s=2, a=2)
         for a in range(2):
             turn_back(1, a)
-            second_product(1, a)
-            res = sb.tile([P, 2, 256], F32, name="res%d" % a)
-            nc.scalar.copy(out=res[:, 0, :], in_=out_banks[a][0][:, 0:256])
-            if a == 0:
-                nc.scalar.copy(out=res[:, 1, :], in_=out_banks[a][1][:, 0:256])
-            else:
-                nc.vector.tensor_copy(out=res[:, 1, :], in_=out_banks[a][1][:, 0:256])
-            nc.sync.dma_start(out=out_view[:, a, :, :], in_=res[:])
+        out_banks = [[bank_tile(6 - 4 * a + s, [P, 256]) for s in range(2)] for a in range(2)]
+        for a in range(2):
+            second_product(0, a, out_banks[a])
+            quantise_z(1, a)
+            second_product(1, a, out_banks[a])
+            for s in range(2):
+                res = sb.tile([P, 256], F32, name="res%d_%d" % (a, s))
+                if s == 0:
+                    nc.scalar.copy(out=res[:], in_=out_banks[a][s][:])
+                else:
+                    nc.vector.tensor_copy(out=res[:], in_=out_banks[a][s][:])
+                nc.sync.dma_start(out=out_view[:, a, s, :], in_=res[:])

@@ -41,7 +41,7 @@ def tile_picked_unet_relu_p_kernel(
             sb.tile([P, PASSES, 4, P], F32, name="w1_raw%d" % c, tag="raw%d" % c, align_bytes=64) for c in range(TILES)
         ]
         skip_sb = [sb.tile([P, U], F32, name="skip_sb%d" % c) for c in range(TILES)]
-        up = [sb.tile([P, U], F32, name="up%d" % c) for c in range(TILES)]
+        up = [sb.tile([P, U], F32, name="up%d" % c, tag="up%d" % c) for c in range(TILES)]
 
         def load_x(z, pieces):
             words = x_words[z].rearrange("p n t -> p (n t)").bitcast(I32)
@@ -127,9 +127,9 @@ def tile_picked_unet_relu_p_kernel(
                 out=xg[1][:, HALF * a : HALF * (a + 1)], in_=x_table[1][:].indirect(offs_sb[:, 16 * a : 16 * (a + 1)])
             )
 
-        def first_product(c, a):
-            bank = bank_tile(a, [P, HALF])
-            cols = slice(HALF * a, HALF * (a + 1))
+        def first_product(c, b, first, count):
+            bank = bank_tile(b, [P, count])
+            cols = slice(first, first + count)
             for z in range(PASSES):
                 nc.tensor.matmul_mx(
                     out=bank[:],
@@ -214,27 +214,48 @@ def tile_picked_unet_relu_p_kernel(
 
         sum_bank = [4, 6, 4, 6]
         sums = {}
-        for c in range(TILES - 1):
-            banks = [first_product(c, a) for a in range(2)]
-            h_a = sb.tile([P, HALF], F32, name="h_a%d" % c)
-            nc.scalar.activation(out=h_a[:], in_=banks[0][:], func=ACT.Relu)
-            scatter(c, 0, h_a)
-            cast_w1(c + 1, c == 0)
-            quantise_w1(c + 1)
-            h_b = sb.tile([P, HALF], F32, name="h_b%d" % c, tag="raw%d" % (c + 1), align_bytes=64)
-            nc.scalar.activation(out=h_b[:], in_=banks[1][:], func=ACT.Relu)
-            if c > 0:
-                turn_up(c - 1, sums[c - 1])
-            scatter(c, HALF, h_b)
-            if c < 2:
-                sums[c] = turn_skip(c, sum_bank[c])
+
+        def relu(values, bank):
+            nc.scalar.activation(out=values, in_=bank, func=ACT.Relu)
+
+        QUARTER = S // 4
+        banks = [first_product(0, 0, 0, QUARTER), first_product(0, 2, QUARTER, QUARTER), first_product(0, 1, HALF, HALF)]
+        for i in range(2):
+            h_q = sb.tile([P, QUARTER], F32, name="h_q%d" % i)
+            relu(h_q[:], banks[i][:])
+            scatter(0, QUARTER * i, h_q)
+        cast_w1(1, True)
+        quantise_w1(1)
+        h_b = sb.tile([P, HALF], F32, name="h_b0", tag="raw1", align_bytes=64)
+        relu(h_b[:], banks[2][:])
+        scatter(0, HALF, h_b)
+        sums[0] = turn_skip(0, sum_bank[0])
+
+        banks = [first_product(1, a, HALF * a, HALF) for a in range(2)]
+        h_a = sb.tile([P, HALF], F32, name="h_a1")
+        relu(h_a[:], banks[0][:])
+        scatter(1, 0, h_a)
+        cast_w1(2, False)
+        quantise_w1(2)
+        h_b = sb.tile([P, HALF], F32, name="h_b1", tag="raw2", align_bytes=64)
+        relu(h_b[:], banks[1][:])
+        turn_up(0, sums[0])
+        scatter(1, HALF, h_b)
+        sums[1] = turn_skip(1, sum_bank[1])
+
+        bank = first_product(2, 0, 0, S)
+        cast_w1(3, False)
+        quantise_w1(3)
+        h_w = sb.tile([P, S], F32, name="h_w2", tag="raw3", align_bytes=64)
+        relu(h_w[:], bank[:])
+        scatter(2, 0, h_w)
+        turn_up(1, sums[1])
 
         c = TILES - 1
-        banks = [first_product(c, a) for a in range(2)]
-        h_last = sb.tile([P, S], F32, name="h_last")
-        for a in range(2):
-            nc.scalar.activation(out=h_last[:, HALF * a : HALF * (a + 1)], in_=banks[a][:], func=ACT.Relu)
-        scatter(c, 0, h_last)
+        bank = first_product(c, 1, 0, S)
+        h_w = sb.tile([P, S], F32, name="h_w3")
+        relu(h_w[:], bank[:])
+        scatter(c, 0, h_w)
         for a in range(2):
             turn_back(0, a)
         sums[2] = turn_skip(2, sum_bank[2])

@@ -43,10 +43,10 @@ def tile_picked_unet_relu_p_kernel(
         skip_sb = [sb.tile([P, U], F32, name="skip_sb%d" % c) for c in range(TILES)]
         up = [sb.tile([P, U], F32, name="up%d" % c, tag="up%d" % c) for c in range(TILES)]
 
-        def load_x(z, pieces):
+        def load_x(z, pieces, which):
             words = x_words[z].rearrange("p n t -> p (n t)").bitcast(I32)
             width = T // pieces
-            for i in range(pieces):
+            for i in which:
                 cols = slice(width * i, width * (i + 1))
                 nc.sync.dma_start(out=x_table[z][:, cols].bitcast(I32), in_=words[:, cols])
 
@@ -71,9 +71,10 @@ def tile_picked_unet_relu_p_kernel(
                 nc.sync.dma_start(out=w2_plane[32 * q : 32 * q + 4, :, :].bitcast(I32), in_=w2_srows[q % 2].bitcast(I32))
 
         nc.vector.memset(xs_table[:].bitcast(I32), 0)
+        load_x(0, 4, range(1))
         nc.sync.dma_start(offs_sb[:], offs)
         nc.sync.dma_start(cell_sb[:], cell)
-        load_x(0, 4)
+        load_x(0, 4, range(1, 4))
         load_w1(0)
         for q in range(4):
             nc.sync.dma_start(
@@ -82,7 +83,7 @@ def tile_picked_unet_relu_p_kernel(
         make_identity(nc, ident[:])
         nc.gpsimd.memset(w2_codes[:].bitcast(I32), 0)
         nc.gpsimd.memset(w2_plane[:].bitcast(I32), 0)
-        load_x(1, 1)
+        load_x(1, 1, range(1))
         load_w1(1)
         load_skip(0)
         load_w1(2)
@@ -147,12 +148,11 @@ def tile_picked_unet_relu_p_kernel(
             nc.vector.tensor_copy(out=up[c][:].indirect(cell_sb[:, first // 16 : (first + count) // 16]), in_=values[:])
 
         zt = [
-            [sb.tile([P, 1024], BF16, name="zt%d_%d" % (g, a), tag="zt%d_%d" % (g, a), align_bytes=64) for a in range(2)]
-            for g in range(2)
+            {a: sb.tile([P, 1024], BF16, name="zt%d_%d" % (g, a), align_bytes=64) for a in range(g, 2)} for g in range(2)
         ]
 
         def turn(banks, src, first):
-            for a in range(2):
+            for a in range(len(banks)):
                 for i in range(4):
                     vb = 4 * (i % 2) + 2 * a + i // 2
                     nc.tensor.matmul(
@@ -164,35 +164,35 @@ def tile_picked_unet_relu_p_kernel(
                         is_transpose=True,
                     )
 
-        def turn_skip(c, b):
-            banks = [bank_tile(b + a, [P, 4, P]) for a in range(2)]
+        def turn_skip(c, b, halves=2):
+            banks = [bank_tile(b + a, [P, 4, P]) for a in range(halves)]
             turn(banks, skip_sb[c], True)
             return banks
 
         def turn_up(c, banks):
             turn(banks, up[c], False)
-            for a in range(2):
+            for a in range(len(banks)):
                 w0 = 32 * (c % 2)
                 dst = zt[c // 2][a][:].rearrange("p (u i w e) -> p i u w e", u=2, i=4, e=2)[:, :, :, w0 : w0 + 32, :]
                 src = banks[a][:].rearrange("p i (w u e) -> p i u w e", u=2, e=2)
-                if c == 3 and a == 1:
-                    nc.vector.tensor_copy(out=dst, in_=src)
-                else:
-                    nc.scalar.copy(out=dst, in_=src)
+                nc.scalar.copy(out=dst, in_=src)
 
         z_bf = [[sb.tile([P, 1024], BF16, name="z_bf%d_%d" % (g, a), align_bytes=64) for a in range(2)] for g in range(2)]
 
         def turn_back(g, a):
             bank = bank_tile(2 + a, [P, 2, 2, P])
-            words = zt[g][a][:].bitcast(F32)
             for q in range(2):
                 for u in range(2):
-                    w0 = 256 * u + P * q
-                    nc.tensor.transpose(bank[:, q, u, :], words[:, w0 : w0 + P], ident[:])
+                    if (g, a) == (1, 0):
+                        words = ztq[q][:].bitcast(F32)[:, P * u : P * (u + 1)]
+                    else:
+                        w0 = 256 * u + P * q
+                        words = zt[g][a][:].bitcast(F32)[:, w0 : w0 + P]
+                    nc.tensor.transpose(bank[:, q, u, :], words, ident[:])
             dst = z_bf[g][a][:].bitcast(F32).rearrange("p (q v u) -> p q v u", q=2, u=2)
             nc.scalar.copy(out=dst, in_=bank[:].rearrange("p q u v -> p q v u"))
 
-        z_codes = [sb.tile([P, 512], U32, name="z_codes%d" % g, align_bytes=64) for g in range(2)]
+        z_codes = {1: sb.tile([P, 512], U32, name="z_codes1", align_bytes=64)}
         z_plane = [sb.tile([P, 512], U8, name="z_plane%d" % g, align_bytes=64) for g in range(2)]
 
         def quantise_z(g, a):
@@ -258,17 +258,66 @@ def tile_picked_unet_relu_p_kernel(
         scatter(c, 0, h_w)
         for a in range(2):
             turn_back(0, a)
+        ztq = [sb.tile([P, 512], BF16, name="ztq%d" % q, align_bytes=64) for q in range(2)]
+
+        def copy_quarter(c, q, blocks):
+            w0 = 32 * (c % 2)
+            dst = ztq[q][:].rearrange("p (u s w e) -> p s u w e", u=2, s=2, e=2)[:, :, :, w0 : w0 + 32, :]
+            nc.scalar.copy(out=dst, in_=blocks.rearrange("p s (w u e) -> p s u w e", u=2, e=2))
+
         sums[2] = turn_skip(2, sum_bank[2])
-        turn_up(2, sums[2])
-        sums[3] = turn_skip(3, sum_bank[3])
+        turn(sums[2], up[2], False)
+        for q in range(2):
+            copy_quarter(2, q, sums[2][0][:, 2 * q : 2 * q + 2, :])
+        dst = zt[1][1][:].rearrange("p (u i w e) -> p i u w e", u=2, i=4, e=2)[:, :, :, 0:32, :]
+        nc.scalar.copy(out=dst, in_=sums[2][1][:].rearrange("p i (w u e) -> p i u w e", u=2, e=2))
+        quarter = [bank_tile(6 + q, [P, 2, P]) for q in range(2)]
+        for src, first in ((skip_sb[c], True), (up[c], False)):
+            for q in range(2):
+                for s in range(2):
+                    vb = 4 * s + q
+                    nc.tensor.matmul(
+                        quarter[q][:, s, :],
+                        src[:, P * vb : P * (vb + 1)],
+                        ident[:],
+                        start=(first and s == 0),
+                        stop=(not first and s == 1),
+                        is_transpose=True,
+                    )
+        for q in range(2):
+            copy_quarter(c, q, quarter[q][:])
+        pair_bank = [0, 1]
+        pairs = sb.tile([P, 2, P, 2], BF16, name="pairs", tag="pairs", align_bytes=64)
+        up_view = up[c][:].rearrange("p (s a e j) -> p a s j e", s=2, a=2, e=2)[:, 1]
+        skip_view = skip_sb[c][:].rearrange("p (s a e j) -> p a s j e", s=2, a=2, e=2)[:, 1]
+        nc.vector.tensor_tensor(out=pairs[:], in0=up_view, in1=skip_view, op=mybir.AluOpType.add)
+        words = pairs[:].rearrange("p s j e -> p (s j e)").bitcast(F32)
+        for s in range(2):
+            bank = bank_tile(pair_bank[s], [P, P])
+            nc.tensor.transpose(bank[:], words[:, P * s : P * (s + 1)], ident[:])
+            dst = zt[1][1][:].rearrange("p (u q s w e) -> p s u q w e", u=2, q=2, s=2, e=2)[:, s, :, :, 32:64, :]
+            src = bank[:].bitcast(BF16).rearrange("p (w u e q) -> p u q w e", u=2, e=2, q=2)
+            if s == 0:
+                nc.vector.tensor_copy(out=dst, in_=src)
+            else:
+                nc.scalar.copy(out=dst, in_=src)
+        z_codes[0] = sb.tile([P, 512], U32, name="z_codes0", tag="pairs", align_bytes=64)
         for a in range(2):
             quantise_z(0, a)
-        turn_up(3, sums[3])
 
         out_view = out.rearrange("m (s a v) -> m a s v", s=2, a=2)
-        for a in range(2):
-            turn_back(1, a)
-        out_banks = [[bank_tile(6 - 4 * a + s, [P, 256]) for s in range(2)] for a in range(2)]
+        turn_back(1, 0)
+        for q in range(2):
+            bank = bank_tile(3 + q, [P, 2, P])
+            for u in range(2):
+                w0 = 256 * u + P * q
+                nc.tensor.transpose(bank[:, u, :], zt[1][1][:].bitcast(F32)[:, w0 : w0 + P], ident[:])
+            dst = z_bf[1][1][:].bitcast(F32)[:, 256 * q : 256 * (q + 1)].rearrange("p (v u) -> p v u", u=2)
+            if q == 0:
+                nc.vector.tensor_copy(out=dst, in_=bank[:].rearrange("p u v -> p v u"))
+            else:
+                nc.scalar.copy(out=dst, in_=bank[:].rearrange("p u v -> p v u"))
+        out_banks = [[bank_tile(b, [P, 256]) for b in pair] for pair in (pair_bank, [2, 3])]
         for a in range(2):
             second_product(0, a, out_banks[a])
             quantise_z(1, a)

@@ -50,10 +50,10 @@ def tile_picked_unet_relu_p_kernel(
                 cols = slice(width * i, width * (i + 1))
                 nc.sync.dma_start(out=x_table[z][:, cols].bitcast(I32), in_=words[:, cols])
 
-        def load_w1(c):
+        def load_w1(c, queue):
             for z in range(PASSES):
                 rows = w1[512 * z : 512 * (z + 1), P * c : P * (c + 1)]
-                nc.sync.dma_start(out=w1_raw[c][:, z, :, :], in_=rows.rearrange("(p j) m -> p j m", j=4))
+                queue.dma_start(out=w1_raw[c][:, z, :, :], in_=rows.rearrange("(p j) m -> p j m", j=4))
 
         def load_skip(c):
             nc.sync.dma_start(out=skip_sb[c][:], in_=skip[P * c : P * (c + 1), :])
@@ -75,7 +75,7 @@ def tile_picked_unet_relu_p_kernel(
         nc.sync.dma_start(offs_sb[:], offs)
         nc.sync.dma_start(cell_sb[:], cell)
         load_x(0, 4, range(1, 4))
-        load_w1(0)
+        load_w1(0, nc.scalar)
         for q in range(4):
             nc.sync.dma_start(
                 out=xs_table[32 * q : 32 * q + 8, :].bitcast(I32), in_=x_scales[:, 4 * q : 4 * q + 4, :].bitcast(I32)
@@ -84,11 +84,11 @@ def tile_picked_unet_relu_p_kernel(
         nc.gpsimd.memset(w2_codes[:].bitcast(I32), 0)
         nc.gpsimd.memset(w2_plane[:].bitcast(I32), 0)
         load_x(1, 1, range(1))
-        load_w1(1)
+        load_w1(1, nc.sync)
         load_skip(0)
-        load_w1(2)
+        load_w1(2, nc.sync)
         load_skip(1)
-        load_w1(3)
+        load_w1(3, nc.sync)
         load_skip(2)
         load_skip(3)
         load_w2()

@@ -288,9 +288,11 @@ def tile_picked_unet_relu_p_kernel(
             copy_quarter(c, q, quarter[q][:])
         pair_bank = [0, 1]
         pairs = sb.tile([P, 2, P, 2], BF16, name="pairs", tag="pairs", align_bytes=64)
-        up_view = up[c][:].rearrange("p (s a e j) -> p a s j e", s=2, a=2, e=2)[:, 1]
-        skip_view = skip_sb[c][:].rearrange("p (s a e j) -> p a s j e", s=2, a=2, e=2)[:, 1]
-        nc.vector.tensor_tensor(out=pairs[:], in0=up_view, in1=skip_view, op=mybir.AluOpType.add)
+        up_view = up[c][:].rearrange("p (s a e g i) -> p a s g e i", s=2, a=2, e=2, i=4)[:, 1]
+        skip_view = skip_sb[c][:].rearrange("p (s a e g i) -> p a s g e i", s=2, a=2, e=2, i=4)[:, 1]
+        for s in range(2):
+            dst = pairs[:, s].rearrange("p (g i) e -> p g e i", i=4)
+            nc.vector.tensor_tensor(out=dst, in0=up_view[:, s], in1=skip_view[:, s], op=mybir.AluOpType.add)
         words = pairs[:].rearrange("p s j e -> p (s j e)").bitcast(F32)
         for s in range(2):
             bank = bank_tile(pair_bank[s], [P, P])

@@ -30,6 +30,11 @@ def tile_picked_unet_relu_p_kernel(
         sb = ctx.enter_context(tc.tile_pool(name="sb", bufs=1))
         ps = ctx.enter_context(tc.psum_pool(name="ps", bufs=1))
 
+        shared = ctx.enter_context(tc.tile_pool(name="shared", bufs=1))
+
+        def placed(name, shape, dtype, offset):
+            return shared.tile(shape, dtype, name=name, offset=offset, align_bytes=64)
+
         def bank_tile(b, shape):
             return ps.tile(shape, F32, name="bank%d" % b, tag="bank%d" % b)
 
@@ -38,8 +43,9 @@ def tile_picked_unet_relu_p_kernel(
         x_table = [sb.tile([P, T], U32, name="x_table%d" % z) for z in range(PASSES)]
         xs_table = sb.tile([P, T], U8, name="xs_table")
         w1_raw = [
-            sb.tile([P, PASSES, 4, P], F32, name="w1_raw%d" % c, tag="raw%d" % c, align_bytes=64) for c in range(TILES)
+            sb.tile([P, PASSES, 4, P], F32, name="w1_raw%d" % c, tag="raw%d" % c, align_bytes=64) for c in range(TILES - 1)
         ]
+        w1_raw.append(placed("w1_raw3", [P, PASSES, 4, P], F32, 1024))
         skip_sb = [sb.tile([P, U], F32, name="skip_sb%d" % c) for c in range(TILES)]
         up = [sb.tile([P, U], F32, name="up%d" % c, tag="up%d" % c) for c in range(TILES)]
 
@@ -96,11 +102,12 @@ def tile_picked_unet_relu_p_kernel(
         for c in range(TILES):
             nc.vector.memset(up[c][:], 0.0)
 
-        w1_bf = [sb.tile([P, PASSES, P * 4], BF16, name="w1_bf%d" % c, align_bytes=64) for c in range(TILES)]
+        w1_bf = {}
         w1_codes = [sb.tile([P, PASSES * P], U32, name="w1_codes%d" % c, align_bytes=64) for c in range(TILES)]
         w1_plane = [sb.tile([P, PASSES * P], U8, name="w1_plane%d" % c, align_bytes=64) for c in range(TILES)]
 
         def cast_w1(c, whole):
+            w1_bf[c] = sb.tile([P, PASSES, P * 4], BF16, name="w1_bf%d" % c, tag="bf%d" % min(c, 2), align_bytes=64)
             if whole:
                 dst = w1_bf[c][:].rearrange("p z (g i j) -> p z g j i", i=4, j=4)
                 src = w1_raw[c][:].rearrange("p z j (g i) -> p z g j i", i=4)
@@ -148,7 +155,8 @@ def tile_picked_unet_relu_p_kernel(
             nc.vector.tensor_copy(out=up[c][:].indirect(cell_sb[:, first // 16 : (first + count) // 16]), in_=values[:])
 
         zt = [
-            {a: sb.tile([P, 1024], BF16, name="zt%d_%d" % (g, a), align_bytes=64) for a in range(g, 2)} for g in range(2)
+            {a: placed("zt0_%d" % a, [P, 1024], BF16, 4096 * a) for a in range(2)},
+            {1: sb.tile([P, 1024], BF16, name="zt1_1", align_bytes=64)},
         ]
 
         def turn(banks, src, first):
@@ -232,21 +240,19 @@ def tile_picked_unet_relu_p_kernel(
         sums[0] = turn_skip(0, sum_bank[0])
 
         banks = [first_product(1, a, HALF * a, HALF) for a in range(2)]
-        h_a = sb.tile([P, HALF], F32, name="h_a1")
-        relu(h_a[:], banks[0][:])
-        scatter(1, 0, h_a)
         cast_w1(2, False)
         quantise_w1(2)
-        h_b = sb.tile([P, HALF], F32, name="h_b1", tag="raw2", align_bytes=64)
-        relu(h_b[:], banks[1][:])
+        h_w = sb.tile([P, S], F32, name="h_w1", tag="raw2", align_bytes=64)
+        for a in range(2):
+            relu(h_w[:, HALF * a : HALF * (a + 1)], banks[a][:])
+        scatter(1, 0, h_w)
+        cast_w1(3, False)
+        quantise_w1(3)
         turn_up(0, sums[0])
-        scatter(1, HALF, h_b)
         sums[1] = turn_skip(1, sum_bank[1])
 
         bank = first_product(2, 0, 0, S)
-        cast_w1(3, False)
-        quantise_w1(3)
-        h_w = sb.tile([P, S], F32, name="h_w2", tag="raw3", align_bytes=64)
+        h_w = placed("h_w2", [P, S], F32, 2048)
         relu(h_w[:], bank[:])
         scatter(2, 0, h_w)
         turn_up(1, sums[1])

@@ -1,7 +1,6 @@
 from contextlib import ExitStack
 
 import concourse.mybir as mybir
-from concourse.masks import make_identity
 
 K, T, S, H, N, U = 1024, 2048, 512, 512, 128, 1024
 FLOPS = 2 * K * H * S + 2 * H * N * U
@@ -17,8 +16,11 @@ ACT = mybir.ActivationFunctionType
 
 P = 128
 PASSES = K // 512
-TILES = H // P
-HALF = S // 2
+PLANES = 4
+FIRST = 128
+CAST_SPLIT = 80
+CHUNK = 256
+CHUNKS = U // CHUNK
 
 
 def tile_picked_unet_relu_p_kernel(
@@ -30,310 +32,223 @@ def tile_picked_unet_relu_p_kernel(
         sb = ctx.enter_context(tc.tile_pool(name="sb", bufs=1))
         ps = ctx.enter_context(tc.psum_pool(name="ps", bufs=1))
 
-        shared = ctx.enter_context(tc.tile_pool(name="shared", bufs=1))
-
-        def placed(name, shape, dtype, offset):
-            return shared.tile(shape, dtype, name=name, offset=offset, align_bytes=64)
-
-        def bank_tile(b, shape):
-            return ps.tile(shape, F32, name="bank%d" % b, tag="bank%d" % b)
+        def bank_tile(b, width):
+            return ps.tile([P, width], F32, name="bank%d" % b, tag="bank%d" % b)
 
         offs_sb = lists.tile([P, S // 16], U16, name="offs_sb")
         cell_sb = lists.tile([P, S // 16], U16, name="cell_sb")
         x_table = [sb.tile([P, T], U32, name="x_table%d" % z) for z in range(PASSES)]
         xs_table = sb.tile([P, T], U8, name="xs_table")
-        w1_raw = [
-            sb.tile([P, PASSES, 4, P], F32, name="w1_raw%d" % c, tag="raw%d" % c, align_bytes=64) for c in range(TILES - 1)
-        ]
-        w1_raw.append(placed("w1_raw3", [P, PASSES, 4, P], F32, 1024))
-        skip_sb = [sb.tile([P, U], F32, name="skip_sb%d" % c) for c in range(TILES)]
-        up = [sb.tile([P, U], F32, name="up%d" % c, tag="up%d" % c) for c in range(TILES)]
+        w1_raw = [sb.tile([P, 4, H], F32, name="w1_raw%d" % z, tag="raw%d" % z) for z in range(PASSES)]
+        up = [sb.tile([P, U], F32, name="up%d" % t) for t in range(PLANES)]
 
-        def load_x(z, pieces, which):
+        def load_x(z, first, count):
             words = x_words[z].rearrange("p n t -> p (n t)").bitcast(I32)
-            width = T // pieces
-            for i in which:
-                cols = slice(width * i, width * (i + 1))
-                nc.sync.dma_start(out=x_table[z][:, cols].bitcast(I32), in_=words[:, cols])
+            cols = slice(first, first + count)
+            nc.sync.dma_start(out=x_table[z][:, cols].bitcast(I32), in_=words[:, cols])
 
-        def load_w1(c, queue):
-            for z in range(PASSES):
-                rows = w1[512 * z : 512 * (z + 1), P * c : P * (c + 1)]
-                queue.dma_start(out=w1_raw[c][:, z, :, :], in_=rows.rearrange("(p j) m -> p j m", j=4))
+        def load_w1(z, first, count):
+            rows = w1[512 * z : 512 * (z + 1), :].rearrange("(p j) m -> p j m", j=4)
+            nc.sync.dma_start(out=w1_raw[z][:, first : first + count, :], in_=rows[:, first : first + count, :])
 
-        def load_skip(c):
-            nc.sync.dma_start(out=skip_sb[c][:], in_=skip[P * c : P * (c + 1), :])
-
-        ident = sb.tile([P, P], F32, name="ident")
-        w2_codes = sb.tile([P, 2, 2, N], U32, name="w2_codes", align_bytes=64)
-        w2_plane = sb.tile([P, 2, N], U8, name="w2_plane", align_bytes=64)
-
-        def load_w2():
-            w2_rows = w2_words[0].rearrange("(h l) c t -> l h (c t)", h=2).bitcast(I32)
-            for s in range(2):
-                nc.sync.dma_start(out=w2_codes[64 * s : 64 * (s + 1), s, :, :].bitcast(I32), in_=w2_rows)
-            w2_srows = w2_scales[0].rearrange("(h a r) c -> a r h c", h=2, a=2)
-            for q in range(4):
-                nc.sync.dma_start(out=w2_plane[32 * q : 32 * q + 4, :, :].bitcast(I32), in_=w2_srows[q % 2].bitcast(I32))
-
+        w2_codes = sb.tile([P, N], U32, name="w2_codes", align_bytes=64)
         nc.vector.memset(xs_table[:].bitcast(I32), 0)
-        load_x(0, 4, range(1))
+        load_x(0, 0, T // 4)
         nc.sync.dma_start(offs_sb[:], offs)
         nc.sync.dma_start(cell_sb[:], cell)
-        load_x(0, 4, range(1, 4))
-        load_w1(0, nc.scalar)
+        nc.sync.dma_start(out=w2_codes[:].bitcast(I32), in_=w2_words[0].rearrange("p n t -> p (n t)").bitcast(I32))
+        for i in range(1, 4):
+            load_x(0, i * T // 4, T // 4)
+        load_w1(0, 0, 2)
         for q in range(4):
             nc.sync.dma_start(
                 out=xs_table[32 * q : 32 * q + 8, :].bitcast(I32), in_=x_scales[:, 4 * q : 4 * q + 4, :].bitcast(I32)
             )
-        make_identity(nc, ident[:])
-        nc.gpsimd.memset(w2_codes[:].bitcast(I32), 0)
-        nc.gpsimd.memset(w2_plane[:].bitcast(I32), 0)
-        load_x(1, 1, range(1))
-        load_w1(1, nc.sync)
-        load_skip(0)
-        load_w1(2, nc.sync)
-        load_skip(1)
-        load_w1(3, nc.sync)
-        load_skip(2)
-        load_skip(3)
-        load_w2()
+        load_w1(0, 2, 2)
+        load_w1(1, 0, 4)
+        load_x(1, 0, T)
+        for t in range(PLANES - 1):
+            nc.vector.memset(up[t][:], 0.0)
+        nc.scalar.activation(out=up[PLANES - 1][:], in_=up[0][:], func=ACT.Copy)
 
-        for c in range(TILES):
-            nc.vector.memset(up[c][:], 0.0)
+        w1_bf = [
+            sb.tile([P, PLANES, P, 4], BF16, name="w1_bf%d" % z, tag="bf%d" % z, align_bytes=64) for z in range(PASSES)
+        ]
+        w1_codes = [sb.tile([P, H], U32, name="w1_codes%d" % z, align_bytes=64) for z in range(PASSES)]
+        w1_plane = [sb.tile([P, H], U8, name="w1_plane%d" % z, align_bytes=64) for z in range(PASSES)]
 
-        w1_bf = {}
-        w1_codes = [sb.tile([P, PASSES * P], U32, name="w1_codes%d" % c, align_bytes=64) for c in range(TILES)]
-        w1_plane = [sb.tile([P, PASSES * P], U8, name="w1_plane%d" % c, align_bytes=64) for c in range(TILES)]
+        def cast_w1(z):
+            dst = w1_bf[z][:].rearrange("p t m j -> p m j t")
+            src = w1_raw[z][:].rearrange("p j (m t) -> p m j t", t=4)
+            nc.vector.tensor_copy(out=dst[:, :CAST_SPLIT], in_=src[:, :CAST_SPLIT])
+            nc.scalar.activation(out=dst[:, CAST_SPLIT:], in_=src[:, CAST_SPLIT:], func=ACT.Copy)
 
-        def cast_w1(c, whole):
-            w1_bf[c] = sb.tile([P, PASSES, P * 4], BF16, name="w1_bf%d" % c, tag="bf%d" % min(c, 2), align_bytes=64)
-            if whole:
-                dst = w1_bf[c][:].rearrange("p z (g i j) -> p z g j i", i=4, j=4)
-                src = w1_raw[c][:].rearrange("p z j (g i) -> p z g j i", i=4)
-                nc.scalar.copy(out=dst, in_=src)
-                return
-            for z in range(PASSES):
-                dst = w1_bf[c][:, z, :].rearrange("p (g i j) -> p g j i", i=4, j=4)
-                src = w1_raw[c][:, z, :, :].rearrange("p j (g i) -> p g j i", i=4)
-                nc.scalar.activation(out=dst, in_=src, func=ACT.Copy)
-
-        def quantise_w1(c):
+        def quantise_w1(z):
             nc.vector.quantize_mx(
-                out=w1_codes[c][:].bitcast(FP8X4), scales=w1_plane[c][:], in_=w1_bf[c][:].rearrange("p z n -> p (z n)")
+                out=w1_codes[z][:].bitcast(FP8X4), scales=w1_plane[z][:], in_=w1_bf[z][:].rearrange("p t m j -> p (t m j)")
             )
 
-        xg = [sb.tile([P, S], U32, name="xg%d" % z, align_bytes=64) for z in range(PASSES)]
+        xg0 = sb.tile([P, S], U32, name="xg0", align_bytes=64)
+        xg1_first = sb.tile([P, FIRST], U32, name="xg1_first", align_bytes=64)
+        xg1_rest = sb.tile([P, S - FIRST], U32, name="xg1_rest", align_bytes=64)
         xg_plane = sb.tile([P, S], U8, name="xg_plane", align_bytes=64)
 
-        cast_w1(0, False)
-        nc.vector.tensor_copy(out=xg[0][:], in_=x_table[0][:].indirect(offs_sb[:]))
+        def entries(tile, first, count):
+            return tile[:, first // 16 : (first + count) // 16]
+
+        nc.vector.tensor_copy(out=xg0[:], in_=x_table[0][:].indirect(offs_sb[:]))
         nc.vector.tensor_copy(out=xg_plane[:], in_=xs_table[:].indirect(offs_sb[:]))
-        quantise_w1(0)
-        for a in range(2):
-            nc.vector.tensor_copy(
-                out=xg[1][:, HALF * a : HALF * (a + 1)], in_=x_table[1][:].indirect(offs_sb[:, 16 * a : 16 * (a + 1)])
+        for z in range(PASSES):
+            cast_w1(z)
+            quantise_w1(z)
+        nc.vector.tensor_copy(out=xg1_first[:], in_=x_table[1][:].indirect(entries(offs_sb, 0, FIRST)))
+        nc.vector.tensor_copy(out=xg1_rest[:], in_=x_table[1][:].indirect(entries(offs_sb, FIRST, S - FIRST)))
+
+        skip_sb = [sb.tile([P, 2, U], F32, name="skip_sb%d" % u, tag="raw%d" % u) for u in range(2)]
+        skip_rows = skip.rearrange("(p j) v -> p j v", j=4)
+        for u in range(2):
+            nc.sync.dma_start(out=skip_sb[u][:], in_=skip_rows[:, 2 * u : 2 * u + 2, :])
+        w2_plane = sb.tile([P, N], U8, name="w2_plane", tag="bf1", align_bytes=64)
+        nc.vector.memset(w2_plane[:].bitcast(I32), 0)
+        for q in range(4):
+            nc.sync.dma_start(
+                out=w2_plane[32 * q : 32 * q + 4, :].bitcast(I32), in_=w2_scales[0, 4 * q : 4 * q + 4, :].bitcast(I32)
             )
 
-        def first_product(c, b, first, count):
-            bank = bank_tile(b, [P, count])
-            cols = slice(first, first + count)
-            for z in range(PASSES):
-                nc.tensor.matmul_mx(
-                    out=bank[:],
-                    lhsT=w1_codes[c][:, P * z : P * (z + 1)].bitcast(FP8X4),
-                    lhsT_scale=w1_plane[c][:, P * z : P * (z + 1)],
-                    rhs=xg[z][:, cols].bitcast(FP8X4),
-                    rhs_scale=xg_plane[4 * z : P, cols],
-                    start=(z == 0),
-                    stop=(z == PASSES - 1),
-                )
-            return bank
-
-        def scatter(c, first, values):
-            count = values.shape[1]
-            nc.vector.tensor_copy(out=up[c][:].indirect(cell_sb[:, first // 16 : (first + count) // 16]), in_=values[:])
-
-        zt = [
-            {a: placed("zt0_%d" % a, [P, 1024], BF16, 4096 * a) for a in range(2)},
-            {1: sb.tile([P, 1024], BF16, name="zt1_1", align_bytes=64)},
+        parts = [
+            (1, 0, FIRST),
+            (0, 0, FIRST),
+            (2, 0, FIRST),
+            (0, FIRST, S - FIRST),
+            (2, FIRST, S - FIRST),
+            (1, FIRST, S - FIRST),
+            (3, 0, S // 2),
+            (3, S // 2, S // 2),
         ]
+        banks = {}
 
-        def turn(banks, src, first):
-            for a in range(len(banks)):
-                for i in range(4):
-                    vb = 4 * (i % 2) + 2 * a + i // 2
-                    nc.tensor.matmul(
-                        banks[a][:, i, :],
-                        src[:, P * vb : P * (vb + 1)],
-                        ident[:],
-                        start=(first and i == 0),
-                        stop=(not first and i == 3),
-                        is_transpose=True,
-                    )
+        def runs(first, count):
+            cuts = [c for c in (0, FIRST, 2 * FIRST, S) if first <= c <= first + count]
+            return list(zip(cuts[:-1], cuts[1:]))
 
-        def turn_skip(c, b, halves=2):
-            banks = [bank_tile(b + a, [P, 4, P]) for a in range(halves)]
-            turn(banks, skip_sb[c], True)
-            return banks
-
-        def turn_up(c, banks):
-            turn(banks, up[c], False)
-            for a in range(len(banks)):
-                w0 = 32 * (c % 2)
-                dst = zt[c // 2][a][:].rearrange("p (u i w e) -> p i u w e", u=2, i=4, e=2)[:, :, :, w0 : w0 + 32, :]
-                src = banks[a][:].rearrange("p i (w u e) -> p i u w e", u=2, e=2)
-                nc.scalar.copy(out=dst, in_=src)
-
-        z_bf = [[sb.tile([P, 1024], BF16, name="z_bf%d_%d" % (g, a), align_bytes=64) for a in range(2)] for g in range(2)]
-
-        def turn_back(g, a):
-            bank = bank_tile(2 + a, [P, 2, 2, P])
-            for q in range(2):
-                for u in range(2):
-                    if (g, a) == (1, 0):
-                        words = ztq[q][:].bitcast(F32)[:, P * u : P * (u + 1)]
+        for z in range(PASSES):
+            for b, (t, first, count) in enumerate(parts):
+                if z == 0:
+                    banks[t, first] = bank_tile(b, count)
+                cuts = runs(first, count)
+                if z == 0 and count == S // 2:
+                    cuts = [(first, first + count)]
+                for i, (lo, hi) in enumerate(cuts):
+                    if z == 0:
+                        words = xg0[:, lo:hi]
+                    elif lo < FIRST:
+                        words = xg1_first[:]
                     else:
-                        w0 = 256 * u + P * q
-                        words = zt[g][a][:].bitcast(F32)[:, w0 : w0 + P]
-                    nc.tensor.transpose(bank[:, q, u, :], words, ident[:])
-            dst = z_bf[g][a][:].bitcast(F32).rearrange("p (q v u) -> p q v u", q=2, u=2)
-            nc.scalar.copy(out=dst, in_=bank[:].rearrange("p q u v -> p q v u"))
-
-        z_codes = {1: sb.tile([P, 512], U32, name="z_codes1", align_bytes=64)}
-        z_plane = [sb.tile([P, 512], U8, name="z_plane%d" % g, align_bytes=64) for g in range(2)]
-
-        def quantise_z(g, a):
-            cols = slice(256 * a, 256 * (a + 1))
-            nc.vector.quantize_mx(out=z_codes[g][:, cols].bitcast(FP8X4), scales=z_plane[g][:, cols], in_=z_bf[g][a][:])
-
-        def second_product(g, a, banks):
-            cols = slice(256 * a, 256 * (a + 1))
-            for s in range(2):
-                nc.tensor.matmul_mx(
-                    out=banks[s][:],
-                    lhsT=w2_codes[:, s, g, :].bitcast(FP8X4),
-                    lhsT_scale=w2_plane[:, g, :],
-                    rhs=z_codes[g][:, cols].bitcast(FP8X4),
-                    rhs_scale=z_plane[g][:, cols],
-                    start=(g == 0),
-                    stop=(g == 1),
-                )
-
-        sum_bank = [4, 6, 4, 6]
-        sums = {}
-
-        def relu(values, bank):
-            nc.scalar.activation(out=values, in_=bank, func=ACT.Relu)
-
-        QUARTER = S // 4
-        banks = [first_product(0, 0, 0, QUARTER), first_product(0, 2, QUARTER, QUARTER), first_product(0, 1, HALF, HALF)]
-        for i in range(2):
-            h_q = sb.tile([P, QUARTER], F32, name="h_q%d" % i)
-            relu(h_q[:], banks[i][:])
-            scatter(0, QUARTER * i, h_q)
-        cast_w1(1, True)
-        quantise_w1(1)
-        h_b = sb.tile([P, HALF], F32, name="h_b0", tag="raw1", align_bytes=64)
-        relu(h_b[:], banks[2][:])
-        scatter(0, HALF, h_b)
-        sums[0] = turn_skip(0, sum_bank[0])
-
-        banks = [first_product(1, a, HALF * a, HALF) for a in range(2)]
-        cast_w1(2, False)
-        quantise_w1(2)
-        h_w = sb.tile([P, S], F32, name="h_w1", tag="raw2", align_bytes=64)
-        for a in range(2):
-            relu(h_w[:, HALF * a : HALF * (a + 1)], banks[a][:])
-        scatter(1, 0, h_w)
-        cast_w1(3, False)
-        quantise_w1(3)
-        turn_up(0, sums[0])
-        sums[1] = turn_skip(1, sum_bank[1])
-
-        bank = first_product(2, 0, 0, S)
-        h_w = placed("h_w2", [P, S], F32, 2048)
-        relu(h_w[:], bank[:])
-        scatter(2, 0, h_w)
-        turn_up(1, sums[1])
-
-        c = TILES - 1
-        bank = first_product(c, 1, 0, S)
-        h_w = sb.tile([P, S], F32, name="h_w3")
-        relu(h_w[:], bank[:])
-        scatter(c, 0, h_w)
-        for a in range(2):
-            turn_back(0, a)
-        ztq = [sb.tile([P, 512], BF16, name="ztq%d" % q, align_bytes=64) for q in range(2)]
-
-        def copy_quarter(c, q, blocks):
-            w0 = 32 * (c % 2)
-            dst = ztq[q][:].rearrange("p (u s w e) -> p s u w e", u=2, s=2, e=2)[:, :, :, w0 : w0 + 32, :]
-            nc.scalar.copy(out=dst, in_=blocks.rearrange("p s (w u e) -> p s u w e", u=2, e=2))
-
-        sums[2] = turn_skip(2, sum_bank[2])
-        turn(sums[2], up[2], False)
-        for q in range(2):
-            copy_quarter(2, q, sums[2][0][:, 2 * q : 2 * q + 2, :])
-        dst = zt[1][1][:].rearrange("p (u i w e) -> p i u w e", u=2, i=4, e=2)[:, :, :, 0:32, :]
-        nc.scalar.copy(out=dst, in_=sums[2][1][:].rearrange("p i (w u e) -> p i u w e", u=2, e=2))
-        quarter = [bank_tile(6 + q, [P, 2, P]) for q in range(2)]
-        for src, first in ((skip_sb[c], True), (up[c], False)):
-            for q in range(2):
-                for s in range(2):
-                    vb = 4 * s + q
-                    nc.tensor.matmul(
-                        quarter[q][:, s, :],
-                        src[:, P * vb : P * (vb + 1)],
-                        ident[:],
-                        start=(first and s == 0),
-                        stop=(not first and s == 1),
-                        is_transpose=True,
+                        words = xg1_rest[:, lo - FIRST : hi - FIRST]
+                    nc.tensor.matmul_mx(
+                        out=banks[t, first][:, lo - first : hi - first],
+                        lhsT=w1_codes[z][:, P * t : P * (t + 1)].bitcast(FP8X4),
+                        lhsT_scale=w1_plane[z][:, P * t : P * (t + 1)],
+                        rhs=words.bitcast(FP8X4),
+                        rhs_scale=xg_plane[4 * z : P, lo:hi],
+                        start=(z == 0 and i == 0),
+                        stop=(z == PASSES - 1 and i == len(cuts) - 1),
                     )
-        for q in range(2):
-            copy_quarter(c, q, quarter[q][:])
-        pair_bank = [0, 1]
-        pairs = sb.tile([P, 2, P, 2], BF16, name="pairs", tag="pairs", align_bytes=64)
-        up_view = up[c][:].rearrange("p (s a e g i) -> p a s g e i", s=2, a=2, e=2, i=4)[:, 1]
-        skip_view = skip_sb[c][:].rearrange("p (s a e g i) -> p a s g e i", s=2, a=2, e=2, i=4)[:, 1]
-        for s in range(2):
-            dst = pairs[:, s].rearrange("p (g i) e -> p g e i", i=4)
-            nc.vector.tensor_tensor(out=dst, in0=up_view[:, s], in1=skip_view[:, s], op=mybir.AluOpType.add)
-        words = pairs[:].rearrange("p s j e -> p (s j e)").bitcast(F32)
-        for s in range(2):
-            bank = bank_tile(pair_bank[s], [P, P])
-            nc.tensor.transpose(bank[:], words[:, P * s : P * (s + 1)], ident[:])
-            dst = zt[1][1][:].rearrange("p (u q s w e) -> p s u q w e", u=2, q=2, s=2, e=2)[:, s, :, :, 32:64, :]
-            src = bank[:].bitcast(BF16).rearrange("p (w u e q) -> p u q w e", u=2, e=2, q=2)
-            if s == 0:
+
+        h = {}
+
+        def relu(t, first, tag=None):
+            count = banks[t, first].shape[1]
+            h[t, first] = sb.tile([P, count], F32, name="h%d_%d" % (t, first), tag=tag or "h%d_%d" % (t, first))
+            nc.scalar.activation(out=h[t, first][:], in_=banks[t, first][:], func=ACT.Relu)
+
+        def scatter(t, first, on_vector, lo=0, hi=None):
+            values = h[t, first][:, lo:hi]
+            window = up[t][:].indirect(entries(cell_sb, first + lo, values.shape[1]))
+            if on_vector:
+                nc.vector.tensor_copy(out=window, in_=values)
+            else:
+                nc.scalar.activation(out=window, in_=values, func=ACT.Copy)
+
+        relu(1, 0)
+        relu(0, 0)
+        scatter(0, 0, True)
+        relu(2, 0)
+        scatter(2, 0, True)
+        scatter(1, 0, False)
+        relu(0, FIRST)
+        scatter(0, FIRST, True)
+        relu(2, FIRST)
+        scatter(2, FIRST, False, 0, FIRST)
+        scatter(2, FIRST, True, FIRST, None)
+        relu(1, FIRST)
+        scatter(1, FIRST, False)
+        relu(3, 0)
+        relu(3, S // 2)
+        scatter(3, 0, False)
+        scatter(3, S // 2, False)
+
+
+        z_rows = sb.tile([P, PLANES, U], BF16, name="z_rows", align_bytes=64)
+
+        def add_skip(t, first, count):
+            cols = slice(first, first + count)
+            nc.vector.tensor_tensor(
+                out=z_rows[:, t, cols], in0=up[t][:, cols], in1=skip_sb[t // 2][:, t % 2, cols], op=mybir.AluOpType.add
+            )
+
+        z_bf = [sb.tile([P, CHUNK, 4], BF16, name="z_bf%d" % c, align_bytes=64) for c in range(CHUNKS)]
+        z_codes = [sb.tile([P, CHUNK], U32, name="z_codes%d" % c, align_bytes=64) for c in range(CHUNKS)]
+        z_plane = [sb.tile([P, CHUNK], U8, name="z_plane%d" % c, align_bytes=64) for c in range(CHUNKS)]
+
+        def interleave(c, first, count, on_vector):
+            dst = z_bf[c][:, first : first + count, :].rearrange("p (g i) t -> p g t i", i=4)
+            src = z_rows[:, :, CHUNK * c + first : CHUNK * c + first + count].rearrange("p t (g i) -> p g t i", i=4)
+            if on_vector:
                 nc.vector.tensor_copy(out=dst, in_=src)
             else:
                 nc.scalar.copy(out=dst, in_=src)
-        z_codes[0] = sb.tile([P, 512], U32, name="z_codes0", tag="pairs", align_bytes=64)
-        for a in range(2):
-            quantise_z(0, a)
 
-        out_view = out.rearrange("m (s a v) -> m a s v", s=2, a=2)
-        turn_back(1, 0)
-        for q in range(2):
-            bank = bank_tile(3 + q, [P, 2, P])
-            for u in range(2):
-                w0 = 256 * u + P * q
-                nc.tensor.transpose(bank[:, u, :], zt[1][1][:].bitcast(F32)[:, w0 : w0 + P], ident[:])
-            dst = z_bf[1][1][:].bitcast(F32)[:, 256 * q : 256 * (q + 1)].rearrange("p (v u) -> p v u", u=2)
-            if q == 0:
-                nc.vector.tensor_copy(out=dst, in_=bank[:].rearrange("p u v -> p v u"))
+        def quantise_z(c):
+            nc.vector.quantize_mx(
+                out=z_codes[c][:].bitcast(FP8X4), scales=z_plane[c][:], in_=z_bf[c][:].rearrange("p v t -> p (v t)")
+            )
+
+        def second_product(c, on_vector):
+            bank = bank_tile(c, CHUNK)
+            nc.tensor.matmul_mx(
+                out=bank[:],
+                lhsT=w2_codes[:].bitcast(FP8X4),
+                lhsT_scale=w2_plane[:],
+                rhs=z_codes[c][:].bitcast(FP8X4),
+                rhs_scale=z_plane[c][:],
+                start=True,
+                stop=True,
+            )
+            res = sb.tile([P, CHUNK], F32, name="res%d" % c)
+            if on_vector:
+                nc.vector.tensor_copy(out=res[:], in_=bank[:])
             else:
-                nc.scalar.copy(out=dst, in_=bank[:].rearrange("p u v -> p v u"))
-        out_banks = [[bank_tile(b, [P, 256]) for b in pair] for pair in (pair_bank, [2, 3])]
-        for a in range(2):
-            second_product(0, a, out_banks[a])
-            quantise_z(1, a)
-            second_product(1, a, out_banks[a])
-            for s in range(2):
-                res = sb.tile([P, 256], F32, name="res%d_%d" % (a, s))
-                if s == 0:
-                    nc.scalar.copy(out=res[:], in_=out_banks[a][s][:])
-                else:
-                    nc.vector.tensor_copy(out=res[:], in_=out_banks[a][s][:])
-                nc.sync.dma_start(out=out_view[:, a, s, :], in_=res[:])
+                nc.scalar.copy(out=res[:], in_=bank[:])
+            nc.sync.dma_start(out=out[:, CHUNK * c : CHUNK * (c + 1)], in_=res[:])
+
+        for t in (0, 2, 1):
+            add_skip(t, 0, U)
+        last = PLANES - 1
+        add_skip(last, 0, CHUNK)
+        interleave(0, 0, CHUNK, False)
+        add_skip(last, 2 * CHUNK, CHUNK)
+        add_skip(last, CHUNK, CHUNK)
+        interleave(1, 0, CHUNK, False)
+        interleave(2, 0, CHUNK, True)
+        add_skip(last, 3 * CHUNK, CHUNK)
+        interleave(3, 0, CHUNK // 4, False)
+        quantise_z(0)
+        interleave(3, CHUNK // 4, 3 * CHUNK // 4, True)
+        second_product(0, False)
+        quantise_z(2)
+        second_product(2, False)
+        quantise_z(1)
+        second_product(1, False)
+        quantise_z(3)
+        second_product(3, True)

@@ -19,8 +19,6 @@ PASSES = K // 512
 PLANES = 4
 FIRST = 128
 CAST_SPLIT = 80
-CHUNK = 256
-CHUNKS = U // CHUNK
 
 
 def tile_picked_unet_relu_p_kernel(
@@ -52,13 +50,10 @@ def tile_picked_unet_relu_p_kernel(
             nc.sync.dma_start(out=w1_raw[z][:, first : first + count, :], in_=rows[:, first : first + count, :])
 
         w2_codes = sb.tile([P, N], U32, name="w2_codes", align_bytes=64)
-        nc.vector.memset(xs_table[:].bitcast(I32), 0)
-        load_x(0, 0, T // 4)
+        nc.gpsimd.memset(xs_table[:].bitcast(I32), 0)
         nc.sync.dma_start(offs_sb[:], offs)
+        load_x(0, 0, T)
         nc.sync.dma_start(cell_sb[:], cell)
-        nc.sync.dma_start(out=w2_codes[:].bitcast(I32), in_=w2_words[0].rearrange("p n t -> p (n t)").bitcast(I32))
-        for i in range(1, 4):
-            load_x(0, i * T // 4, T // 4)
         load_w1(0, 0, 2)
         for q in range(4):
             nc.sync.dma_start(
@@ -67,17 +62,17 @@ def tile_picked_unet_relu_p_kernel(
         load_w1(0, 2, 2)
         load_w1(1, 0, 4)
         load_x(1, 0, T)
+        nc.sync.dma_start(out=w2_codes[:].bitcast(I32), in_=w2_words[0].rearrange("p n t -> p (n t)").bitcast(I32))
         for t in range(PLANES - 1):
             nc.vector.memset(up[t][:], 0.0)
         nc.scalar.activation(out=up[PLANES - 1][:], in_=up[0][:], func=ACT.Copy)
 
-        w1_bf = [
-            sb.tile([P, PLANES, P, 4], BF16, name="w1_bf%d" % z, tag="bf%d" % z, align_bytes=64) for z in range(PASSES)
-        ]
+        w1_bf = {}
         w1_codes = [sb.tile([P, H], U32, name="w1_codes%d" % z, align_bytes=64) for z in range(PASSES)]
         w1_plane = [sb.tile([P, H], U8, name="w1_plane%d" % z, align_bytes=64) for z in range(PASSES)]
 
         def cast_w1(z):
+            w1_bf[z] = sb.tile([P, PLANES, P, 4], BF16, name="w1_bf%d" % z, tag="bf", align_bytes=64)
             dst = w1_bf[z][:].rearrange("p t m j -> p m j t")
             src = w1_raw[z][:].rearrange("p j (m t) -> p m j t", t=4)
             nc.vector.tensor_copy(out=dst[:, :CAST_SPLIT], in_=src[:, :CAST_SPLIT])
@@ -108,7 +103,7 @@ def tile_picked_unet_relu_p_kernel(
         skip_rows = skip.rearrange("(p j) v -> p j v", j=4)
         for u in range(2):
             nc.sync.dma_start(out=skip_sb[u][:], in_=skip_rows[:, 2 * u : 2 * u + 2, :])
-        w2_plane = sb.tile([P, N], U8, name="w2_plane", tag="bf1", align_bytes=64)
+        w2_plane = sb.tile([P, N], U8, name="w2_plane", tag="bf", align_bytes=64)
         nc.vector.memset(w2_plane[:].bitcast(I32), 0)
         for q in range(4):
             nc.sync.dma_start(
@@ -178,7 +173,7 @@ def tile_picked_unet_relu_p_kernel(
         scatter(1, 0, False)
         relu(0, FIRST)
         scatter(0, FIRST, True)
-        relu(2, FIRST)
+        relu(2, FIRST, tag="rows")
         scatter(2, FIRST, False, 0, FIRST)
         scatter(2, FIRST, True, FIRST, None)
         relu(1, FIRST)
@@ -189,7 +184,7 @@ def tile_picked_unet_relu_p_kernel(
         scatter(3, S // 2, False)
 
 
-        z_rows = sb.tile([P, PLANES, U], BF16, name="z_rows", align_bytes=64)
+        z_rows = sb.tile([P, PLANES, U], BF16, name="z_rows", tag="rows")
 
         def add_skip(t, first, count):
             cols = slice(first, first + count)
@@ -197,13 +192,15 @@ def tile_picked_unet_relu_p_kernel(
                 out=z_rows[:, t, cols], in0=up[t][:, cols], in1=skip_sb[t // 2][:, t % 2, cols], op=mybir.AluOpType.add
             )
 
-        z_bf = [sb.tile([P, CHUNK, 4], BF16, name="z_bf%d" % c, align_bytes=64) for c in range(CHUNKS)]
-        z_codes = [sb.tile([P, CHUNK], U32, name="z_codes%d" % c, align_bytes=64) for c in range(CHUNKS)]
-        z_plane = [sb.tile([P, CHUNK], U8, name="z_plane%d" % c, align_bytes=64) for c in range(CHUNKS)]
+        chunks = [(0, 256), (256, 256), (512, 256), (768, 128), (896, 128)]
+        z_bf = [sb.tile([P, n, 4], BF16, name="z_bf%d" % c, align_bytes=64) for c, (v, n) in enumerate(chunks)]
+        z_codes = [sb.tile([P, n], U32, name="z_codes%d" % c, align_bytes=64) for c, (v, n) in enumerate(chunks)]
+        z_plane = [sb.tile([P, n], U8, name="z_plane%d" % c, align_bytes=64) for c, (v, n) in enumerate(chunks)]
 
-        def interleave(c, first, count, on_vector):
-            dst = z_bf[c][:, first : first + count, :].rearrange("p (g i) t -> p g t i", i=4)
-            src = z_rows[:, :, CHUNK * c + first : CHUNK * c + first + count].rearrange("p t (g i) -> p g t i", i=4)
+        def interleave(c, on_vector, lo=0, hi=None):
+            first, count = chunks[c]
+            dst = z_bf[c][:, lo:hi, :].rearrange("p (g i) t -> p g t i", i=4)
+            src = z_rows[:, :, first : first + count][:, :, lo:hi].rearrange("p t (g i) -> p g t i", i=4)
             if on_vector:
                 nc.vector.tensor_copy(out=dst, in_=src)
             else:
@@ -215,7 +212,8 @@ def tile_picked_unet_relu_p_kernel(
             )
 
         def second_product(c, on_vector):
-            bank = bank_tile(c, CHUNK)
+            first, count = chunks[c]
+            bank = bank_tile(c, count)
             nc.tensor.matmul_mx(
                 out=bank[:],
                 lhsT=w2_codes[:].bitcast(FP8X4),
@@ -225,30 +223,31 @@ def tile_picked_unet_relu_p_kernel(
                 start=True,
                 stop=True,
             )
-            res = sb.tile([P, CHUNK], F32, name="res%d" % c)
+            res = sb.tile([P, count], F32, name="res%d" % c)
             if on_vector:
                 nc.vector.tensor_copy(out=res[:], in_=bank[:])
             else:
                 nc.scalar.copy(out=res[:], in_=bank[:])
-            nc.sync.dma_start(out=out[:, CHUNK * c : CHUNK * (c + 1)], in_=res[:])
+            nc.sync.dma_start(out=out[:, first : first + count], in_=res[:])
 
-        for t in (0, 2, 1):
+        for t in range(PLANES - 1):
             add_skip(t, 0, U)
         last = PLANES - 1
-        add_skip(last, 0, CHUNK)
-        interleave(0, 0, CHUNK, False)
-        add_skip(last, 2 * CHUNK, CHUNK)
-        add_skip(last, CHUNK, CHUNK)
-        interleave(1, 0, CHUNK, False)
-        interleave(2, 0, CHUNK, True)
-        add_skip(last, 3 * CHUNK, CHUNK)
-        interleave(3, 0, CHUNK // 4, False)
+        add_skip(last, 0, 256)
+        interleave(0, False)
+        add_skip(last, 256, 512)
+        interleave(2, False)
+        add_skip(last, 768, 256)
+        interleave(1, True)
+        interleave(4, False)
         quantise_z(0)
-        interleave(3, CHUNK // 4, 3 * CHUNK // 4, True)
+        interleave(3, True)
         second_product(0, False)
-        quantise_z(2)
-        second_product(2, False)
         quantise_z(1)
         second_product(1, False)
+        quantise_z(2)
+        second_product(2, False)
         quantise_z(3)
         second_product(3, True)
+        quantise_z(4)
+        second_product(4, True)

@@ -19,6 +19,7 @@ PASSES = K // 512
 PLANES = 4
 FIRST = 128
 CAST_SPLIT = 80
+EARLY = 5
 
 
 def tile_picked_unet_relu_p_kernel(
@@ -52,15 +53,15 @@ def tile_picked_unet_relu_p_kernel(
         w2_codes = sb.tile([P, N], U32, name="w2_codes", align_bytes=64)
         nc.gpsimd.memset(xs_table[:].bitcast(I32), 0)
         nc.sync.dma_start(offs_sb[:], offs)
-        load_x(0, 0, T)
+        load_w1(0, 0, 4)
         nc.sync.dma_start(cell_sb[:], cell)
-        load_w1(0, 0, 2)
+        load_w1(1, 0, 2)
         for q in range(4):
             nc.sync.dma_start(
                 out=xs_table[32 * q : 32 * q + 8, :].bitcast(I32), in_=x_scales[:, 4 * q : 4 * q + 4, :].bitcast(I32)
             )
-        load_w1(0, 2, 2)
-        load_w1(1, 0, 4)
+        load_w1(1, 2, 2)
+        load_x(0, 0, T)
         load_x(1, 0, T)
         nc.sync.dma_start(out=w2_codes[:].bitcast(I32), in_=w2_words[0].rearrange("p n t -> p (n t)").bitcast(I32))
         for t in range(PLANES - 1):
@@ -83,21 +84,21 @@ def tile_picked_unet_relu_p_kernel(
                 out=w1_codes[z][:].bitcast(FP8X4), scales=w1_plane[z][:], in_=w1_bf[z][:].rearrange("p t m j -> p (t m j)")
             )
 
-        xg0 = sb.tile([P, S], U32, name="xg0", align_bytes=64)
-        xg1_first = sb.tile([P, FIRST], U32, name="xg1_first", align_bytes=64)
-        xg1_rest = sb.tile([P, S - FIRST], U32, name="xg1_rest", align_bytes=64)
+        xg_first = [sb.tile([P, FIRST], U32, name="xg_first%d" % z, align_bytes=64) for z in range(PASSES)]
+        xg_rest = [sb.tile([P, S - FIRST], U32, name="xg_rest%d" % z, align_bytes=64) for z in range(PASSES)]
         xg_plane = sb.tile([P, S], U8, name="xg_plane", align_bytes=64)
 
         def entries(tile, first, count):
             return tile[:, first // 16 : (first + count) // 16]
 
-        nc.vector.tensor_copy(out=xg0[:], in_=x_table[0][:].indirect(offs_sb[:]))
+        cast_w1(0)
+        quantise_w1(0)
         nc.vector.tensor_copy(out=xg_plane[:], in_=xs_table[:].indirect(offs_sb[:]))
+        cast_w1(1)
+        quantise_w1(1)
         for z in range(PASSES):
-            cast_w1(z)
-            quantise_w1(z)
-        nc.vector.tensor_copy(out=xg1_first[:], in_=x_table[1][:].indirect(entries(offs_sb, 0, FIRST)))
-        nc.vector.tensor_copy(out=xg1_rest[:], in_=x_table[1][:].indirect(entries(offs_sb, FIRST, S - FIRST)))
+            nc.vector.tensor_copy(out=xg_first[z][:], in_=x_table[z][:].indirect(entries(offs_sb, 0, FIRST)))
+            nc.vector.tensor_copy(out=xg_rest[z][:], in_=x_table[z][:].indirect(entries(offs_sb, FIRST, S - FIRST)))
 
         skip_sb = [sb.tile([P, 2, U], F32, name="skip_sb%d" % u, tag="raw%d" % u) for u in range(2)]
         skip_rows = skip.rearrange("(p j) v -> p j v", j=4)
@@ -126,20 +127,13 @@ def tile_picked_unet_relu_p_kernel(
             cuts = [c for c in (0, FIRST, 2 * FIRST, S) if first <= c <= first + count]
             return list(zip(cuts[:-1], cuts[1:]))
 
-        for z in range(PASSES):
-            for b, (t, first, count) in enumerate(parts):
-                if z == 0:
-                    banks[t, first] = bank_tile(b, count)
-                cuts = runs(first, count)
-                if z == 0 and count == S // 2:
-                    cuts = [(first, first + count)]
+        def first_product(b):
+            t, first, count = parts[b]
+            banks[t, first] = bank_tile(b % EARLY, count)
+            cuts = runs(first, count)
+            for z in range(PASSES):
                 for i, (lo, hi) in enumerate(cuts):
-                    if z == 0:
-                        words = xg0[:, lo:hi]
-                    elif lo < FIRST:
-                        words = xg1_first[:]
-                    else:
-                        words = xg1_rest[:, lo - FIRST : hi - FIRST]
+                    words = xg_first[z][:] if lo < FIRST else xg_rest[z][:, lo - FIRST : hi - FIRST]
                     nc.tensor.matmul_mx(
                         out=banks[t, first][:, lo - first : hi - first],
                         lhsT=w1_codes[z][:, P * t : P * (t + 1)].bitcast(FP8X4),
@@ -149,6 +143,9 @@ def tile_picked_unet_relu_p_kernel(
                         start=(z == 0 and i == 0),
                         stop=(z == PASSES - 1 and i == len(cuts) - 1),
                     )
+
+        for b in range(EARLY):
+            first_product(b)
 
         h = {}
 
@@ -176,6 +173,8 @@ def tile_picked_unet_relu_p_kernel(
         relu(2, FIRST, tag="rows")
         scatter(2, FIRST, False, 0, FIRST)
         scatter(2, FIRST, True, FIRST, None)
+        for b in range(EARLY, len(parts)):
+            first_product(b)
         relu(1, FIRST)
         scatter(1, FIRST, False)
         relu(3, 0)

@@ -30,14 +30,18 @@ def tile_picked_unet_relu_p_kernel(
         lists = ctx.enter_context(tc.tile_pool(name="lists", bufs=1))
         sb = ctx.enter_context(tc.tile_pool(name="sb", bufs=1))
         ps = ctx.enter_context(tc.psum_pool(name="ps", bufs=1))
+        shared = ctx.enter_context(tc.tile_pool(name="shared", bufs=1))
+
+        def placed(name, shape, dtype, offset):
+            return shared.tile(shape, dtype, name=name, offset=offset, align_bytes=64)
 
         def bank_tile(b, width):
             return ps.tile([P, width], F32, name="bank%d" % b, tag="bank%d" % b)
 
         offs_sb = lists.tile([P, S // 16], U16, name="offs_sb")
         cell_sb = lists.tile([P, S // 16], U16, name="cell_sb")
-        x_table = [sb.tile([P, T], U32, name="x_table%d" % z) for z in range(PASSES)]
-        xs_table = sb.tile([P, T], U8, name="xs_table")
+        xs_table = placed("xs_table", [P, T], U8, 0)
+        x_table = [sb.tile([P, T], U32, name="x_table0")]
         w1_raw = [sb.tile([P, 4, H], F32, name="w1_raw%d" % z, tag="raw%d" % z) for z in range(PASSES)]
         up = [sb.tile([P, U], F32, name="up%d" % t) for t in range(PLANES)]
 
@@ -50,30 +54,43 @@ def tile_picked_unet_relu_p_kernel(
             rows = w1[512 * z : 512 * (z + 1), :].rearrange("(p j) m -> p j m", j=4)
             nc.sync.dma_start(out=w1_raw[z][:, first : first + count, :], in_=rows[:, first : first + count, :])
 
-        w2_codes = sb.tile([P, N], U32, name="w2_codes", align_bytes=64)
-        nc.gpsimd.memset(xs_table[:].bitcast(I32), 0)
+        scale_rows = x_scales.rearrange("z q c -> (z q) c")
         nc.sync.dma_start(offs_sb[:], offs)
+        nc.sync.dma_start(out=xs_table[0:32, :].bitcast(I32), in_=scale_rows.bitcast(I32))
         load_w1(0, 0, 4)
-        nc.sync.dma_start(cell_sb[:], cell)
-        load_w1(1, 0, 2)
-        for q in range(4):
-            nc.sync.dma_start(
-                out=xs_table[32 * q : 32 * q + 8, :].bitcast(I32), in_=x_scales[:, 4 * q : 4 * q + 4, :].bitcast(I32)
-            )
-        load_w1(1, 2, 2)
+        load_w1(1, 0, 4)
         load_x(0, 0, T)
+        nc.sync.dma_start(cell_sb[:], cell)
+        nc.vector.memset(xs_table[32:64, :].bitcast(I32), 0)
+        nc.vector.memset(xs_table[64:128, :].bitcast(I32), 0)
+        xs_picked = sb.tile([P, S], U8, name="xs_picked")
+        xg_plane = [sb.tile([P, S], U8, name="xg_plane%d" % z, align_bytes=64) for z in range(PASSES)]
+        for z in range(PASSES):
+            nc.vector.memset(xg_plane[z][:].bitcast(I32), 0)
+        nc.vector.tensor_copy(out=xs_picked[:], in_=xs_table[:].indirect(offs_sb[:]))
+
+        def move_scales(z):
+            for q in range(4):
+                row = 16 * z + 4 * q
+                nc.sync.dma_start(
+                    out=xg_plane[z][32 * q : 32 * q + 4, :].bitcast(I32), in_=xs_picked[row : row + 4, :].bitcast(I32)
+                )
+
+        move_scales(0)
+        x_table.append(placed("x_table1", [P, T], U32, 0))
         load_x(1, 0, T)
-        nc.sync.dma_start(out=w2_codes[:].bitcast(I32), in_=w2_words[0].rearrange("p n t -> p (n t)").bitcast(I32))
-        for t in range(PLANES - 1):
+        move_scales(1)
+        for t in (0, 2):
             nc.vector.memset(up[t][:], 0.0)
-        nc.scalar.activation(out=up[PLANES - 1][:], in_=up[0][:], func=ACT.Copy)
+        for t in (1, 3):
+            nc.scalar.activation(out=up[t][:], in_=up[0][:], func=ACT.Copy)
 
         w1_bf = {}
         w1_codes = [sb.tile([P, H], U32, name="w1_codes%d" % z, align_bytes=64) for z in range(PASSES)]
         w1_plane = [sb.tile([P, H], U8, name="w1_plane%d" % z, align_bytes=64) for z in range(PASSES)]
 
         def cast_w1(z):
-            w1_bf[z] = sb.tile([P, PLANES, P, 4], BF16, name="w1_bf%d" % z, tag="bf", align_bytes=64)
+            w1_bf[z] = placed("w1_bf%d" % z, [P, PLANES, P, 4], BF16, 4 * T)
             dst = w1_bf[z][:].rearrange("p t m j -> p m j t")
             src = w1_raw[z][:].rearrange("p j (m t) -> p m j t", t=4)
             nc.vector.tensor_copy(out=dst[:, :CAST_SPLIT], in_=src[:, :CAST_SPLIT])
@@ -86,14 +103,12 @@ def tile_picked_unet_relu_p_kernel(
 
         xg_first = [sb.tile([P, FIRST], U32, name="xg_first%d" % z, align_bytes=64) for z in range(PASSES)]
         xg_rest = [sb.tile([P, S - FIRST], U32, name="xg_rest%d" % z, align_bytes=64) for z in range(PASSES)]
-        xg_plane = sb.tile([P, S], U8, name="xg_plane", align_bytes=64)
 
         def entries(tile, first, count):
             return tile[:, first // 16 : (first + count) // 16]
 
         cast_w1(0)
         quantise_w1(0)
-        nc.vector.tensor_copy(out=xg_plane[:], in_=xs_table[:].indirect(offs_sb[:]))
         cast_w1(1)
         quantise_w1(1)
         for z in range(PASSES):
@@ -104,8 +119,10 @@ def tile_picked_unet_relu_p_kernel(
         skip_rows = skip.rearrange("(p j) v -> p j v", j=4)
         for u in range(2):
             nc.sync.dma_start(out=skip_sb[u][:], in_=skip_rows[:, 2 * u : 2 * u + 2, :])
-        w2_plane = sb.tile([P, N], U8, name="w2_plane", tag="bf", align_bytes=64)
+        w2_codes = placed("w2_codes", [P, N], U32, 4 * T)
+        w2_plane = placed("w2_plane", [P, N], U8, 4 * T + 4 * N)
         nc.vector.memset(w2_plane[:].bitcast(I32), 0)
+        nc.sync.dma_start(out=w2_codes[:].bitcast(I32), in_=w2_words[0].rearrange("p n t -> p (n t)").bitcast(I32))
         for q in range(4):
             nc.sync.dma_start(
                 out=w2_plane[32 * q : 32 * q + 4, :].bitcast(I32), in_=w2_scales[0, 4 * q : 4 * q + 4, :].bitcast(I32)
@@ -139,7 +156,7 @@ def tile_picked_unet_relu_p_kernel(
                         lhsT=w1_codes[z][:, P * t : P * (t + 1)].bitcast(FP8X4),
                         lhsT_scale=w1_plane[z][:, P * t : P * (t + 1)],
                         rhs=words.bitcast(FP8X4),
-                        rhs_scale=xg_plane[4 * z : P, lo:hi],
+                        rhs_scale=xg_plane[z][:, lo:hi],
                         start=(z == 0 and i == 0),
                         stop=(z == PASSES - 1 and i == len(cuts) - 1),
                     )

@@ -187,9 +187,8 @@ def tile_picked_unet_relu_p_kernel(
         scatter(1, 0, False)
         relu(0, FIRST)
         scatter(0, FIRST, True)
-        relu(2, FIRST, tag="rows")
-        scatter(2, FIRST, False, 0, FIRST)
-        scatter(2, FIRST, True, FIRST, None)
+        relu(2, FIRST, tag="late")
+        scatter(2, FIRST, True)
         for b in range(EARLY, len(parts)):
             first_product(b)
         relu(1, FIRST)
@@ -200,11 +199,12 @@ def tile_picked_unet_relu_p_kernel(
         scatter(3, S // 2, False)
 
 
-        z_rows = sb.tile([P, PLANES, U], BF16, name="z_rows", tag="rows")
+        z_rows = sb.tile([P, PLANES, U], BF16, name="z_rows")
 
         def add_skip(t, first, count):
             cols = slice(first, first + count)
-            nc.vector.tensor_tensor(
+            engine = nc.gpsimd if t == 0 else nc.vector
+            engine.tensor_tensor(
                 out=z_rows[:, t, cols], in0=up[t][:, cols], in1=skip_sb[t // 2][:, t % 2, cols], op=mybir.AluOpType.add
             )
 

@@ -19,7 +19,7 @@ PASSES = K // 512
 PLANES = 4
 FIRST = 128
 CAST_SPLIT = 80
-EARLY = 5
+EARLY = 6
 
 
 def tile_picked_unet_relu_p_kernel(
@@ -132,11 +132,11 @@ def tile_picked_unet_relu_p_kernel(
             (1, 0, FIRST),
             (0, 0, FIRST),
             (2, 0, FIRST),
+            (3, 0, FIRST),
             (0, FIRST, S - FIRST),
             (2, FIRST, S - FIRST),
             (1, FIRST, S - FIRST),
-            (3, 0, S // 2),
-            (3, S // 2, S // 2),
+            (3, FIRST, S - FIRST),
         ]
         banks = {}
 
@@ -187,17 +187,16 @@ def tile_picked_unet_relu_p_kernel(
         scatter(1, 0, False)
         relu(0, FIRST)
         scatter(0, FIRST, True)
-        relu(2, FIRST, tag="late")
+        relu(3, 0)
+        relu(2, FIRST)
         scatter(2, FIRST, True)
+        scatter(3, 0, False)
         for b in range(EARLY, len(parts)):
             first_product(b)
         relu(1, FIRST)
+        relu(3, FIRST)
         scatter(1, FIRST, False)
-        relu(3, 0)
-        relu(3, S // 2)
-        scatter(3, 0, False)
-        scatter(3, S // 2, False)
-
+        scatter(3, FIRST, False)
 
         z_rows = sb.tile([P, PLANES, U], BF16, name="z_rows")
 
@@ -246,18 +245,21 @@ def tile_picked_unet_relu_p_kernel(
                 nc.scalar.copy(out=res[:], in_=bank[:])
             nc.sync.dma_start(out=out[:, first : first + count], in_=res[:])
 
-        for t in range(PLANES - 1):
-            add_skip(t, 0, U)
+        add_skip(0, 0, U)
+        add_skip(1, 0, U)
+        add_skip(2, 0, 768)
         last = PLANES - 1
         add_skip(last, 0, 256)
         interleave(0, False)
         add_skip(last, 256, 512)
         interleave(2, False)
+        add_skip(2, 768, 256)
         add_skip(last, 768, 256)
         interleave(1, True)
+        interleave(3, False, 0, 32)
         interleave(4, False)
         quantise_z(0)
-        interleave(3, True)
+        interleave(3, True, 32, 128)
         second_product(0, False)
         quantise_z(1)
         second_product(1, False)

@@ -129,8 +129,8 @@ def tile_picked_unet_relu_p_kernel(
             )
 
         parts = [
-            (1, 0, FIRST),
             (0, 0, FIRST),
+            (1, 0, FIRST),
             (2, 0, FIRST),
             (3, 0, FIRST),
             (0, FIRST, S - FIRST),
@@ -179,9 +179,9 @@ def tile_picked_unet_relu_p_kernel(
             else:
                 nc.scalar.activation(out=window, in_=values, func=ACT.Copy)
 
-        relu(1, 0)
         relu(0, 0)
         scatter(0, 0, True)
+        relu(1, 0)
         relu(2, 0)
         scatter(2, 0, True)
         scatter(1, 0, False)

@@ -54,32 +54,24 @@ def tile_picked_unet_relu_p_kernel(
             rows = w1[512 * z : 512 * (z + 1), :].rearrange("(p j) m -> p j m", j=4)
             nc.sync.dma_start(out=w1_raw[z][:, first : first + count, :], in_=rows[:, first : first + count, :])
 
-        scale_rows = x_scales.rearrange("z q c -> (z q) c")
         nc.sync.dma_start(offs_sb[:], offs)
-        nc.sync.dma_start(out=xs_table[0:32, :].bitcast(I32), in_=scale_rows.bitcast(I32))
+        nc.sync.dma_start(out=xs_table[96:128, :].bitcast(I32), in_=x_scales.bitcast(I32).rearrange("z q c -> q z c"))
         load_w1(0, 0, 4)
         load_w1(1, 0, 4)
         load_x(0, 0, T)
         nc.sync.dma_start(cell_sb[:], cell)
-        nc.vector.memset(xs_table[32:64, :].bitcast(I32), 0)
-        nc.vector.memset(xs_table[64:128, :].bitcast(I32), 0)
+        nc.vector.memset(xs_table[0:96, :].bitcast(I32), 0)
         xs_picked = sb.tile([P, S], U8, name="xs_picked")
-        xg_plane = [sb.tile([P, S], U8, name="xg_plane%d" % z, align_bytes=64) for z in range(PASSES)]
-        for z in range(PASSES):
-            nc.vector.memset(xg_plane[z][:].bitcast(I32), 0)
+        xg_plane = sb.tile([P, PASSES * S], U8, name="xg_plane", align_bytes=64)
+        nc.vector.memset(xg_plane[:].bitcast(I32), 0)
         nc.vector.tensor_copy(out=xs_picked[:], in_=xs_table[:].indirect(offs_sb[:]))
 
-        def move_scales(z):
-            for q in range(4):
-                row = 16 * z + 4 * q
-                nc.sync.dma_start(
-                    out=xg_plane[z][32 * q : 32 * q + 4, :].bitcast(I32), in_=xs_picked[row : row + 4, :].bitcast(I32)
-                )
-
-        move_scales(0)
+        for q in range(4):
+            nc.sync.dma_start(
+                out=xg_plane[32 * q : 32 * q + 4, :].bitcast(I32), in_=xs_picked[96 + 8 * q : 104 + 8 * q, :].bitcast(I32)
+            )
         x_table.append(placed("x_table1", [P, T], U32, 0))
         load_x(1, 0, T)
-        move_scales(1)
         for t in (0, 2):
             nc.vector.memset(up[t][:], 0.0)
         for t in (1, 3):
@@ -156,7 +148,7 @@ def tile_picked_unet_relu_p_kernel(
                         lhsT=w1_codes[z][:, P * t : P * (t + 1)].bitcast(FP8X4),
                         lhsT_scale=w1_plane[z][:, P * t : P * (t + 1)],
                         rhs=words.bitcast(FP8X4),
-                        rhs_scale=xg_plane[z][:, lo:hi],
+                        rhs_scale=xg_plane[:, S * z + lo : S * z + hi],
                         start=(z == 0 and i == 0),
                         stop=(z == PASSES - 1 and i == len(cuts) - 1),
                     )

@@ -42,7 +42,7 @@ def tile_picked_unet_relu_p_kernel(
         cell_sb = lists.tile([P, S // 16], U16, name="cell_sb")
         xs_table = placed("xs_table", [P, T], U8, 0)
         x_table = [sb.tile([P, T], U32, name="x_table0")]
-        w1_raw = [sb.tile([P, 4, H], F32, name="w1_raw%d" % z, tag="raw%d" % z) for z in range(PASSES)]
+        w1_raw = [placed("w1_raw%d" % z, [P, 4, H], F32, (6 + 4 * z) * T) for z in range(PASSES)]
         up = [sb.tile([P, U], F32, name="up%d" % t) for t in range(PLANES)]
 
         def load_x(z, first, count):
@@ -54,12 +54,14 @@ def tile_picked_unet_relu_p_kernel(
             rows = w1[512 * z : 512 * (z + 1), :].rearrange("(p j) m -> p j m", j=4)
             nc.sync.dma_start(out=w1_raw[z][:, first : first + count, :], in_=rows[:, first : first + count, :])
 
+        load_w1(0, 0, 2)
         nc.sync.dma_start(offs_sb[:], offs)
         nc.sync.dma_start(out=xs_table[96:128, :].bitcast(I32), in_=x_scales.bitcast(I32).rearrange("z q c -> q z c"))
-        load_w1(0, 0, 4)
-        load_w1(1, 0, 4)
-        load_x(0, 0, T)
-        nc.sync.dma_start(cell_sb[:], cell)
+        load_w1(0, 2, 2)
+        load_w1(1, 0, 2)
+        load_w1(1, 2, 2)
+        load_x(0, 0, T // 2)
+        load_x(0, T // 2, T // 2)
         nc.vector.memset(xs_table[0:96, :].bitcast(I32), 0)
         xs_picked = sb.tile([P, S], U8, name="xs_picked")
         xg_plane = sb.tile([P, PASSES * S], U8, name="xg_plane", align_bytes=64)
@@ -72,6 +74,7 @@ def tile_picked_unet_relu_p_kernel(
             )
         x_table.append(placed("x_table1", [P, T], U32, 0))
         load_x(1, 0, T)
+        nc.sync.dma_start(cell_sb[:], cell)
         for t in (0, 2):
             nc.vector.memset(up[t][:], 0.0)
         for t in (1, 3):
@@ -107,10 +110,8 @@ def tile_picked_unet_relu_p_kernel(
             nc.vector.tensor_copy(out=xg_first[z][:], in_=x_table[z][:].indirect(entries(offs_sb, 0, FIRST)))
             nc.vector.tensor_copy(out=xg_rest[z][:], in_=x_table[z][:].indirect(entries(offs_sb, FIRST, S - FIRST)))
 
-        skip_sb = [sb.tile([P, 2, U], F32, name="skip_sb%d" % u, tag="raw%d" % u) for u in range(2)]
-        skip_rows = skip.rearrange("(p j) v -> p j v", j=4)
-        for u in range(2):
-            nc.sync.dma_start(out=skip_sb[u][:], in_=skip_rows[:, 2 * u : 2 * u + 2, :])
+        skip_sb = placed("skip_sb", [P, PLANES, U], F32, 6 * T)
+        nc.sync.dma_start(out=skip_sb[:], in_=skip.rearrange("(p j) v -> p j v", j=4))
         w2_codes = placed("w2_codes", [P, N], U32, 4 * T)
         w2_plane = placed("w2_plane", [P, N], U8, 4 * T + 4 * N)
         nc.vector.memset(w2_plane[:].bitcast(I32), 0)
@@ -196,7 +197,7 @@ def tile_picked_unet_relu_p_kernel(
             cols = slice(first, first + count)
             engine = nc.gpsimd if t == 0 else nc.vector
             engine.tensor_tensor(
-                out=z_rows[:, t, cols], in0=up[t][:, cols], in1=skip_sb[t // 2][:, t % 2, cols], op=mybir.AluOpType.add
+                out=z_rows[:, t, cols], in0=up[t][:, cols], in1=skip_sb[:, t, cols], op=mybir.AluOpType.add
             )
 
         chunks = [(0, 256), (256, 256), (512, 256), (768, 128), (896, 128)]
@@ -218,6 +219,8 @@ def tile_picked_unet_relu_p_kernel(
                 out=z_codes[c][:].bitcast(FP8X4), scales=z_plane[c][:], in_=z_bf[c][:].rearrange("p v t -> p (v t)")
             )
 
+        res = sb.tile([P, U], F32, name="res")
+
         def second_product(c, on_vector):
             first, count = chunks[c]
             bank = bank_tile(c, count)
@@ -230,12 +233,14 @@ def tile_picked_unet_relu_p_kernel(
                 start=True,
                 stop=True,
             )
-            res = sb.tile([P, count], F32, name="res%d" % c)
+            cols = slice(first, first + count)
             if on_vector:
-                nc.vector.tensor_copy(out=res[:], in_=bank[:])
+                nc.vector.tensor_copy(out=res[:, cols], in_=bank[:])
             else:
-                nc.scalar.copy(out=res[:], in_=bank[:])
-            nc.sync.dma_start(out=out[:, first : first + count], in_=res[:])
+                nc.scalar.copy(out=res[:, cols], in_=bank[:])
+            if c > 0:
+                stored = slice(0 if c == 1 else first, first + count)
+                nc.sync.dma_start(out=out[:, stored], in_=res[:, stored])
 
         add_skip(0, 0, U)
         add_skip(1, 0, U)

from contextlib import ExitStack

import concourse.mybir as mybir

K, T, S, H, N, U = 1024, 2048, 512, 512, 128, 1024
FLOPS = 2 * K * H * S + 2 * H * N * U

F32 = mybir.dt.float32
BF16 = mybir.dt.bfloat16
I32 = mybir.dt.int32
U32 = mybir.dt.uint32
U16 = mybir.dt.uint16
U8 = mybir.dt.uint8
FP8X4 = mybir.dt.float8_e4m3fn_x4
ACT = mybir.ActivationFunctionType

P = 128
PASSES = K // 512
PLANES = 4
FIRST = 128
CAST_SPLIT = 80
EARLY = 6


def tile_picked_unet_relu_p_kernel(
    tc, x_words, x_scales, w1, w2_words, w2_scales, skip, offs, cell, out
):
    nc = tc.nc
    with ExitStack() as ctx:
        lists = ctx.enter_context(tc.tile_pool(name="lists", bufs=1))
        sb = ctx.enter_context(tc.tile_pool(name="sb", bufs=1))
        ps = ctx.enter_context(tc.psum_pool(name="ps", bufs=1))
        shared = ctx.enter_context(tc.tile_pool(name="shared", bufs=1))

        def placed(name, shape, dtype, offset):
            return shared.tile(shape, dtype, name=name, offset=offset, align_bytes=64)

        def bank_tile(b, width):
            return ps.tile([P, width], F32, name="bank%d" % b, tag="bank%d" % b)

        offs_sb = lists.tile([P, S // 16], U16, name="offs_sb")
        cell_sb = lists.tile([P, S // 16], U16, name="cell_sb")
        xs_table = placed("xs_table", [P, T], U8, 0)
        x_table = [sb.tile([P, T], U32, name="x_table0")]
        w1_raw = [placed("w1_raw%d" % z, [P, 4, H], F32, (6 + 4 * z) * T) for z in range(PASSES)]
        up = [sb.tile([P, U], F32, name="up%d" % t) for t in range(PLANES)]

        def load_x(z, first, count):
            words = x_words[z].rearrange("p n t -> p (n t)").bitcast(I32)
            cols = slice(first, first + count)
            nc.sync.dma_start(out=x_table[z][:, cols].bitcast(I32), in_=words[:, cols])

        def load_w1(z, first, count):
            rows = w1[512 * z : 512 * (z + 1), :].rearrange("(p j) m -> p j m", j=4)
            nc.sync.dma_start(out=w1_raw[z][:, first : first + count, :], in_=rows[:, first : first + count, :])

        load_w1(0, 0, 2)
        nc.sync.dma_start(offs_sb[:], offs)
        nc.sync.dma_start(out=xs_table[96:128, :].bitcast(I32), in_=x_scales.bitcast(I32).rearrange("z q c -> q z c"))
        load_w1(0, 2, 2)
        load_w1(1, 0, 2)
        load_w1(1, 2, 2)
        load_x(0, 0, T // 2)
        load_x(0, T // 2, T // 2)
        nc.vector.memset(xs_table[0:96, :].bitcast(I32), 0)
        xs_picked = sb.tile([P, S], U8, name="xs_picked")
        xg_plane = sb.tile([P, PASSES * S], U8, name="xg_plane", align_bytes=64)
        nc.vector.memset(xg_plane[:].bitcast(I32), 0)
        nc.vector.tensor_copy(out=xs_picked[:], in_=xs_table[:].indirect(offs_sb[:]))

        for q in range(4):
            nc.sync.dma_start(
                out=xg_plane[32 * q : 32 * q + 4, :].bitcast(I32), in_=xs_picked[96 + 8 * q : 104 + 8 * q, :].bitcast(I32)
            )
        x_table.append(placed("x_table1", [P, T], U32, 0))
        load_x(1, 0, T)
        nc.sync.dma_start(cell_sb[:], cell)
        for t in (0, 2):
            nc.vector.memset(up[t][:], 0.0)
        for t in (1, 3):
            nc.scalar.activation(out=up[t][:], in_=up[0][:], func=ACT.Copy)

        w1_bf = {}
        w1_codes = [sb.tile([P, H], U32, name="w1_codes%d" % z, align_bytes=64) for z in range(PASSES)]
        w1_plane = [sb.tile([P, H], U8, name="w1_plane%d" % z, align_bytes=64) for z in range(PASSES)]

        def cast_w1(z):
            w1_bf[z] = placed("w1_bf%d" % z, [P, PLANES, P, 4], BF16, 4 * T)
            dst = w1_bf[z][:].rearrange("p t m j -> p m j t")
            src = w1_raw[z][:].rearrange("p j (m t) -> p m j t", t=4)
            nc.vector.tensor_copy(out=dst[:, :CAST_SPLIT], in_=src[:, :CAST_SPLIT])
            nc.scalar.activation(out=dst[:, CAST_SPLIT:], in_=src[:, CAST_SPLIT:], func=ACT.Copy)

        def quantise_w1(z):
            nc.vector.quantize_mx(
                out=w1_codes[z][:].bitcast(FP8X4), scales=w1_plane[z][:], in_=w1_bf[z][:].rearrange("p t m j -> p (t m j)")
            )

        xg_first = [sb.tile([P, FIRST], U32, name="xg_first%d" % z, align_bytes=64) for z in range(PASSES)]
        xg_rest = [sb.tile([P, S - FIRST], U32, name="xg_rest%d" % z, align_bytes=64) for z in range(PASSES)]

        def entries(tile, first, count):
            return tile[:, first // 16 : (first + count) // 16]

        cast_w1(0)
        quantise_w1(0)
        cast_w1(1)
        quantise_w1(1)
        for z in range(PASSES):
            nc.vector.tensor_copy(out=xg_first[z][:], in_=x_table[z][:].indirect(entries(offs_sb, 0, FIRST)))
            nc.vector.tensor_copy(out=xg_rest[z][:], in_=x_table[z][:].indirect(entries(offs_sb, FIRST, S - FIRST)))

        skip_sb = placed("skip_sb", [P, PLANES, U], F32, 6 * T)
        nc.sync.dma_start(out=skip_sb[:], in_=skip.rearrange("(p j) v -> p j v", j=4))
        w2_codes = placed("w2_codes", [P, N], U32, 4 * T)
        w2_plane = placed("w2_plane", [P, N], U8, 4 * T + 4 * N)
        nc.vector.memset(w2_plane[:].bitcast(I32), 0)
        nc.sync.dma_start(out=w2_codes[:].bitcast(I32), in_=w2_words[0].rearrange("p n t -> p (n t)").bitcast(I32))
        for q in range(4):
            nc.sync.dma_start(
                out=w2_plane[32 * q : 32 * q + 4, :].bitcast(I32), in_=w2_scales[0, 4 * q : 4 * q + 4, :].bitcast(I32)
            )

        parts = [
            (0, 0, FIRST),
            (1, 0, FIRST),
            (2, 0, FIRST),
            (3, 0, FIRST),
            (0, FIRST, S - FIRST),
            (2, FIRST, S - FIRST),
            (1, FIRST, S - FIRST),
            (3, FIRST, S - FIRST),
        ]
        banks = {}

        def runs(first, count):
            cuts = [c for c in (0, FIRST, 2 * FIRST, S) if first <= c <= first + count]
            return list(zip(cuts[:-1], cuts[1:]))

        def first_product(b):
            t, first, count = parts[b]
            banks[t, first] = bank_tile(b % EARLY, count)
            cuts = runs(first, count)
            for z in range(PASSES):
                for i, (lo, hi) in enumerate(cuts):
                    words = xg_first[z][:] if lo < FIRST else xg_rest[z][:, lo - FIRST : hi - FIRST]
                    nc.tensor.matmul_mx(
                        out=banks[t, first][:, lo - first : hi - first],
                        lhsT=w1_codes[z][:, P * t : P * (t + 1)].bitcast(FP8X4),
                        lhsT_scale=w1_plane[z][:, P * t : P * (t + 1)],
                        rhs=words.bitcast(FP8X4),
                        rhs_scale=xg_plane[:, S * z + lo : S * z + hi],
                        start=(z == 0 and i == 0),
                        stop=(z == PASSES - 1 and i == len(cuts) - 1),
                    )

        for b in range(EARLY):
            first_product(b)

        h = {}

        def relu(t, first, tag=None):
            count = banks[t, first].shape[1]
            h[t, first] = sb.tile([P, count], F32, name="h%d_%d" % (t, first), tag=tag or "h%d_%d" % (t, first))
            nc.scalar.activation(out=h[t, first][:], in_=banks[t, first][:], func=ACT.Relu)

        def scatter(t, first, on_vector, lo=0, hi=None):
            values = h[t, first][:, lo:hi]
            window = up[t][:].indirect(entries(cell_sb, first + lo, values.shape[1]))
            if on_vector:
                nc.vector.tensor_copy(out=window, in_=values)
            else:
                nc.scalar.activation(out=window, in_=values, func=ACT.Copy)

        relu(0, 0)
        scatter(0, 0, True)
        relu(1, 0)
        relu(2, 0)
        scatter(2, 0, True)
        scatter(1, 0, False)
        relu(0, FIRST)
        scatter(0, FIRST, True)
        relu(3, 0)
        relu(2, FIRST)
        scatter(2, FIRST, True)
        scatter(3, 0, False)
        for b in range(EARLY, len(parts)):
            first_product(b)
        relu(1, FIRST)
        relu(3, FIRST)
        scatter(1, FIRST, False)
        scatter(3, FIRST, False)

        z_rows = sb.tile([P, PLANES, U], BF16, name="z_rows")

        def add_skip(t, first, count):
            cols = slice(first, first + count)
            engine = nc.gpsimd if t == 0 else nc.vector
            engine.tensor_tensor(
                out=z_rows[:, t, cols], in0=up[t][:, cols], in1=skip_sb[:, t, cols], op=mybir.AluOpType.add
            )

        chunks = [(0, 256), (256, 256), (512, 256), (768, 128), (896, 128)]
        z_bf = [sb.tile([P, n, 4], BF16, name="z_bf%d" % c, align_bytes=64) for c, (v, n) in enumerate(chunks)]
        z_codes = [sb.tile([P, n], U32, name="z_codes%d" % c, align_bytes=64) for c, (v, n) in enumerate(chunks)]
        z_plane = [sb.tile([P, n], U8, name="z_plane%d" % c, align_bytes=64) for c, (v, n) in enumerate(chunks)]

        def interleave(c, on_vector, lo=0, hi=None):
            first, count = chunks[c]
            dst = z_bf[c][:, lo:hi, :].rearrange("p (g i) t -> p g t i", i=4)
            src = z_rows[:, :, first : first + count][:, :, lo:hi].rearrange("p t (g i) -> p g t i", i=4)
            if on_vector:
                nc.vector.tensor_copy(out=dst, in_=src)
            else:
                nc.scalar.copy(out=dst, in_=src)

        def quantise_z(c):
            nc.vector.quantize_mx(
                out=z_codes[c][:].bitcast(FP8X4), scales=z_plane[c][:], in_=z_bf[c][:].rearrange("p v t -> p (v t)")
            )

        res = sb.tile([P, U], F32, name="res")

        def second_product(c, on_vector):
            first, count = chunks[c]
            bank = bank_tile(c, count)
            nc.tensor.matmul_mx(
                out=bank[:],
                lhsT=w2_codes[:].bitcast(FP8X4),
                lhsT_scale=w2_plane[:],
                rhs=z_codes[c][:].bitcast(FP8X4),
                rhs_scale=z_plane[c][:],
                start=True,
                stop=True,
            )
            cols = slice(first, first + count)
            if on_vector:
                nc.vector.tensor_copy(out=res[:, cols], in_=bank[:])
            else:
                nc.scalar.copy(out=res[:, cols], in_=bank[:])
            if c > 0:
                stored = slice(0 if c == 1 else first, first + count)
                nc.sync.dma_start(out=out[:, stored], in_=res[:, stored])

        add_skip(0, 0, U)
        add_skip(1, 0, U)
        add_skip(2, 0, 768)
        last = PLANES - 1
        add_skip(last, 0, 256)
        interleave(0, False)
        add_skip(last, 256, 512)
        interleave(2, False)
        add_skip(2, 768, 256)
        add_skip(last, 768, 256)
        interleave(1, True)
        interleave(3, False, 0, 32)
        interleave(4, False)
        quantise_z(0)
        interleave(3, True, 32, 128)
        second_product(0, False)
        quantise_z(1)
        second_product(1, False)
        quantise_z(2)
        second_product(2, False)
        quantise_z(3)
        second_product(3, True)
        quantise_z(4)
        second_product(4, True)
